import numpy as np
import ml_dtypes


def mxq(x, axis, fmt="e4m3"):
    dtype, down = {"e4m3": (ml_dtypes.float8_e4m3fn, 7), "e5m2": (ml_dtypes.float8_e5m2, 14)}[fmt]
    v = np.moveaxis(np.asarray(x, np.float32).astype(ml_dtypes.bfloat16).astype(np.float64), axis, -1)
    blocks = v.reshape(v.shape[:-1] + (-1, 32))
    amax = np.abs(blocks).max(-1, keepdims=True)
    byte = np.maximum(np.where(amax > 0, np.frexp(amax)[1] - 1 + 127, 0) - down, 1)
    scale = np.exp2(byte - 127.0)
    codes = (blocks / scale).astype(np.float32).astype(dtype).astype(np.float64)
    return np.moveaxis((codes * scale).reshape(v.shape), -1, axis)


WIDE = False


def mx_kscale(k):
    if not WIDE:
        return np.ones(k)
    levels = np.array([10, -10, 5, -5, 0])
    if k % 512:
        return np.exp2(np.random.permutation(np.resize(levels, k // 32))).repeat(32)
    a = np.empty((k // 512, 16))
    for p in range(k // 512):
        a[p, :8] = np.random.permutation(np.resize(levels, 8))
        for g in range(8):
            far = levels[np.abs(levels - a[p, g]) >= 10]
            a[p, g + 8] = far[np.random.randint(len(far))]
    return np.exp2(a.ravel()).repeat(32)


def f64(x):
    return np.asarray(x).astype(np.float64)


def striped(idx):
    return np.tile(idx.reshape(-1, 16).T, (8, 1)).astype(np.uint16)


def unstriped(offs):
    return offs[:16].T.reshape(-1).astype(np.int64)


def pack_weight(w):
    k, n = w.shape
    w = f64(np.asarray(w, np.float32).astype(ml_dtypes.bfloat16)).reshape(k // 32, 32, n)
    amax = np.abs(w).max(1)
    byte = np.clip(np.where(amax > 0, np.frexp(amax)[1] - 1 + 127 - 7, 1), 1, 254)
    scaled = (w * np.exp2(127.0 - byte)[:, None, :]).reshape(k, n).astype(np.float32)
    words = np.ascontiguousarray(scaled.reshape(k // 512, 128, 4, n).transpose(0, 1, 3, 2)).astype(ml_dtypes.float8_e4m3fn).view(np.uint8)
    return words, np.ascontiguousarray(byte.astype(np.uint8).reshape(k // 512, 16, n))


def unpack_weight(words, scales):
    g, p, n, _ = words.shape
    vals = np.ascontiguousarray(words).view(ml_dtypes.float8_e4m3fn).astype(np.float64) * np.repeat(np.exp2(scales.astype(np.float64) - 127.0), 8, axis=1)[..., None]
    return vals.transpose(0, 1, 3, 2).reshape(g * 512, n)


def gelu(v):
    return 0.5 * v * (1.0 + np.tanh(np.sqrt(2.0 / np.pi) * (v + 0.044715 * v**3)))


K, T, S, H, N, V = 512, 1024, 512, 512, 128, 256


def setup_inputs():
    n = np.random.standard_normal
    s = mx_kscale(K)[:, None]
    u = mx_kscale(H)
    packed_xT = pack_weight(n((K, T)) * s)
    return {
        "x_words": packed_xT[0],
        "x_scales": packed_xT[1],
        "w1": (n((K, H)) / np.sqrt(K) / s * u).astype(np.float32),
        "w2": (n((H, N)) / np.sqrt(H) / u[:, None]).astype(np.float32),
        "meas": (n((N, V))).astype(np.float32),
        "offs": striped(np.random.permutation(T)[:S]),
        "line": striped(np.random.permutation(S)[:V]),
    }


def reference(x_words, x_scales, w1, w2, meas, offs, line):
    xq = unpack_weight(x_words, x_scales)[:, unstriped(offs)]
    h = gelu(mxq(f64(w1), 0, "e4m3").T @ xq)
    y = mxq(f64(w2), 0, "e4m3").T @ mxq(h, 0, "e4m3")
    out = y.copy()
    out[:, unstriped(line)] = 0.25 * y[:, unstriped(line)] + 0.75 * f64(meas)
    return out

@@ -1,0 +1,149 @@
+from contextlib import ExitStack
+
+import concourse.mybir as mybir
+
+K, T, S, H, N, V = 512, 1024, 512, 512, 128, 256
+FLOPS = 2 * K * H * S + 2 * H * N * S
+
+F32 = mybir.dt.float32
+BF16 = mybir.dt.bfloat16
+I32 = mybir.dt.int32
+U32 = mybir.dt.uint32
+U16 = mybir.dt.uint16
+U8 = mybir.dt.uint8
+FP8X4 = mybir.dt.float8_e4m3fn_x4
+GELU = mybir.ActivationFunctionType.Gelu_apprx_tanh
+MULT = mybir.AluOpType.mult
+ADD = mybir.AluOpType.add
+
+P = 128
+PACK = 4
+CHUNK = 128
+CHUNKS = S // CHUNK
+BLOCK = 32
+RUN = BLOCK // PACK
+
+
+def tile_picked_ydcons_gelu_p_kernel(tc, x_words, x_scales, w1, w2, meas, offs, line, out):
+    nc = tc.nc
+    with ExitStack() as ctx:
+        keep = ctx.enter_context(tc.tile_pool(name="keep", bufs=1))
+        psum = ctx.enter_context(tc.psum_pool(name="psum", bufs=1))
+
+        offs_t = keep.tile([P, S // 16], U16, name="offs_t")
+        line_t = keep.tile([P, V // 16], U16, name="line_t")
+        xw = keep.tile([P, T], U32, name="xw", align_bytes=64)
+        xs = keep.tile([P, T], U8, name="xs", tag="chain0", align_bytes=64)
+        w1_raw = keep.tile([P, PACK, H], F32, name="w1_raw", align_bytes=64)
+        warm = keep.tile([P, 1], F32, name="warm", tag="early_late", align_bytes=64)
+        warm_out = keep.tile([P, 1], F32, name="warm_out")
+        quarter = keep.tile([P, V], F32, name="quarter", align_bytes=64)
+
+        nc.vector.memset(xs[:].bitcast(I32), 0)
+        nc.vector.memset(warm[:], 0.0)
+        nc.scalar.activation(out=warm_out[:], in_=warm[:], func=GELU)
+
+        nc.vector.memset(quarter[:], 0.25)
+
+        w1_rows = w1.rearrange("(p j) c -> p j c", j=PACK)
+        nc.sync.dma_start(out=offs_t[:], in_=offs)
+        nc.sync.dma_start(out=w1_raw[:, :1, :], in_=w1_rows[:, :1, :])
+        nc.sync.dma_start(out=line_t[:], in_=line)
+        for q in range(4):
+            nc.sync.dma_start(out=xs[32 * q : 32 * q + 4, :].bitcast(I32), in_=x_scales[0][4 * q : 4 * q + 4, :].bitcast(I32))
+        nc.sync.dma_start(out=w1_raw[:, 1:, :], in_=w1_rows[:, 1:, :])
+        nc.sync.dma_start(out=xw[:].bitcast(I32), in_=x_words[0].rearrange("p n t -> p (n t)").bitcast(I32))
+
+        gs = keep.tile([P, S], U8, name="gs", align_bytes=64)
+        nc.vector.tensor_copy(out=gs[:], in_=xs[:].indirect(offs_t[:]))
+
+        late = keep.tile([P, PACK * N + V], F32, name="late", tag="early_late", align_bytes=64)
+        w2_rows = w2.rearrange("(b t r) n -> t b r n", t=PACK, r=RUN)
+        for t in range(PACK):
+            nc.sync.dma_start(out=late[:, t * N : (t + 1) * N], in_=w2_rows[t])
+        nc.sync.dma_start(out=late[:, PACK * N :], in_=meas)
+
+        gw = []
+        gw_tags = ("chain0", "chain2", "chain3", "chain1")
+
+        def gather(c):
+            gw.append(keep.tile([P, CHUNK], U32, name="gw%d" % c, tag=gw_tags[c], align_bytes=64))
+            nc.vector.tensor_copy(out=gw[c][:], in_=xw[:].indirect(offs_t[:, c * CHUNK // 16 : (c + 1) * CHUNK // 16]))
+
+        w1_codes = [keep.tile([P, P], U32, name="w1_codes%d" % t, align_bytes=64) for t in range(PACK)]
+        w1_scales = [keep.tile([P, P], U8, name="w1_scales%d" % t, align_bytes=64) for t in range(PACK)]
+        w1_bf = [keep.tile([P, P, PACK], BF16, name="w1_bf%d" % t, tag="chain%d" % t, align_bytes=64) for t in range(PACK)]
+        w1_src = w1_raw[:].rearrange("p j (b t r) -> p t b j r", t=PACK, r=RUN)
+
+        def weave_w1(t, copy):
+            copy(out=w1_bf[t][:].rearrange("p (b r) j -> p b j r", r=RUN), in_=w1_src[:, t, :, :, :])
+
+        def quantize_w1(t):
+            nc.vector.quantize_mx(
+                out=w1_codes[t][:].bitcast(FP8X4),
+                scales=w1_scales[t][:],
+                in_=w1_bf[t][:].rearrange("p m j -> p (m j)"),
+            )
+
+        weave_w1(0, nc.vector.tensor_copy)
+        weave_w1(2, nc.scalar.copy)
+        weave_w1(1, nc.vector.tensor_copy)
+        weave_w1(3, nc.scalar.copy)
+        for t in range(PACK - 1):
+            quantize_w1(t)
+        gather(0)
+        quantize_w1(PACK - 1)
+        for c in range(1, CHUNKS):
+            gather(c)
+
+        w2_bf = keep.tile([P, N, PACK], BF16, name="w2_bf", align_bytes=64)
+        w2_codes = keep.tile([P, N], U32, name="w2_codes", align_bytes=64)
+        w2_scales = keep.tile([P, N], U8, name="w2_scales", align_bytes=64)
+        nc.vector.tensor_copy(
+            out=w2_bf[:].rearrange("p (c i) t -> p c t i", i=4),
+            in_=late[:, : PACK * N].rearrange("p (t c i) -> p c t i", t=PACK, i=4),
+        )
+        meas75 = keep.tile([P, V], F32, name="meas75", align_bytes=64)
+        nc.vector.tensor_scalar_mul(out=meas75[:], in0=late[:, PACK * N :], scalar1=0.75)
+        nc.vector.quantize_mx(out=w2_codes[:].bitcast(FP8X4), scales=w2_scales[:], in_=w2_bf[:].rearrange("p n j -> p (n j)"))
+
+        pre = [psum.tile([P, PACK, CHUNK], F32, name="pre%d" % c) for c in range(CHUNKS)]
+        for c in range(CHUNKS):
+            for t in range(PACK):
+                nc.tensor.matmul_mx(
+                    out=pre[c][:, t, :],
+                    lhsT=w1_codes[t][:].bitcast(FP8X4),
+                    lhsT_scale=w1_scales[t][:],
+                    rhs=gw[c][:].bitcast(FP8X4),
+                    rhs_scale=gs[:, c * CHUNK : (c + 1) * CHUNK],
+                    start=True,
+                    stop=True,
+                )
+
+        y = keep.tile([P, S], F32, name="y", align_bytes=64)
+        for c in range(CHUNKS):
+            h_bf = keep.tile([P, CHUNK, PACK], BF16, name="h_bf%d" % c, align_bytes=64)
+            h_codes = keep.tile([P, CHUNK], U32, name="h_codes%d" % c, align_bytes=64)
+            h_scales = keep.tile([P, CHUNK], U8, name="h_scales%d" % c, align_bytes=64)
+            y_acc = psum.tile([P, CHUNK], F32, name="y_acc%d" % c)
+            nc.scalar.activation(out=h_bf[:], in_=pre[c][:].rearrange("p t n -> p n t"), func=GELU)
+            nc.vector.quantize_mx(out=h_codes[:].bitcast(FP8X4), scales=h_scales[:], in_=h_bf[:].rearrange("p n t -> p (n t)"))
+            nc.tensor.matmul_mx(
+                out=y_acc[:],
+                lhsT=w2_codes[:].bitcast(FP8X4),
+                lhsT_scale=w2_scales[:],
+                rhs=h_codes[:].bitcast(FP8X4),
+                rhs_scale=h_scales[:],
+                start=True,
+                stop=True,
+            )
+            cols = slice(c * CHUNK, (c + 1) * CHUNK)
+            if c == CHUNKS - 1:
+                nc.scalar.copy(out=y[:, cols], in_=y_acc[:])
+            else:
+                nc.vector.tensor_copy(out=y[:, cols], in_=y_acc[:])
+
+        picked = keep.tile([P, V], F32, name="picked", align_bytes=64)
+        nc.vector.tensor_tensor(out=picked[:], in0=y[:].indirect(line_t[:]), in1=quarter[:], op=MULT)
+        nc.vector.tensor_tensor(out=y[:].indirect(line_t[:]), in0=picked[:], in1=meas75[:], op=ADD)
+        nc.sync.dma_start(out=out, in_=y[:])

@@ -22,6 +22,8 @@ CHUNK = 128
 CHUNKS = S // CHUNK
 BLOCK = 32
 RUN = BLOCK // PACK
+GROUPS = ((0, 256), (256, 128), (384, 128))
+COPY = mybir.ActivationFunctionType.Copy
 
 
 def tile_picked_ydcons_gelu_p_kernel(tc, x_words, x_scales, w1, w2, meas, offs, line, out):
@@ -37,18 +39,17 @@ def tile_picked_ydcons_gelu_p_kernel(tc, x_words, x_scales, w1, w2, meas, offs, 
         w1_raw = keep.tile([P, PACK, H], F32, name="w1_raw", align_bytes=64)
         warm = keep.tile([P, 1], F32, name="warm", tag="early_late", align_bytes=64)
         warm_out = keep.tile([P, 1], F32, name="warm_out")
-        quarter = keep.tile([P, V], F32, name="quarter", align_bytes=64)
 
         nc.vector.memset(xs[:].bitcast(I32), 0)
         nc.vector.memset(warm[:], 0.0)
         nc.scalar.activation(out=warm_out[:], in_=warm[:], func=GELU)
-
+        quarter = keep.tile([P, V], F32, name="quarter", align_bytes=64)
         nc.vector.memset(quarter[:], 0.25)
+
 
         w1_rows = w1.rearrange("(p j) c -> p j c", j=PACK)
         nc.sync.dma_start(out=offs_t[:], in_=offs)
         nc.sync.dma_start(out=w1_raw[:, :1, :], in_=w1_rows[:, :1, :])
-        nc.sync.dma_start(out=line_t[:], in_=line)
         for q in range(4):
             nc.sync.dma_start(out=xs[32 * q : 32 * q + 4, :].bitcast(I32), in_=x_scales[0][4 * q : 4 * q + 4, :].bitcast(I32))
         nc.sync.dma_start(out=w1_raw[:, 1:, :], in_=w1_rows[:, 1:, :])
@@ -62,6 +63,7 @@ def tile_picked_ydcons_gelu_p_kernel(tc, x_words, x_scales, w1, w2, meas, offs, 
         for t in range(PACK):
             nc.sync.dma_start(out=late[:, t * N : (t + 1) * N], in_=w2_rows[t])
         nc.sync.dma_start(out=late[:, PACK * N :], in_=meas)
+        nc.sync.dma_start(out=line_t[:], in_=line)
 
         gw = []
         gw_tags = ("chain0", "chain2", "chain3", "chain1")
@@ -73,10 +75,13 @@ def tile_picked_ydcons_gelu_p_kernel(tc, x_words, x_scales, w1, w2, meas, offs, 
         w1_codes = [keep.tile([P, P], U32, name="w1_codes%d" % t, align_bytes=64) for t in range(PACK)]
         w1_scales = [keep.tile([P, P], U8, name="w1_scales%d" % t, align_bytes=64) for t in range(PACK)]
         w1_bf = [keep.tile([P, P, PACK], BF16, name="w1_bf%d" % t, tag="chain%d" % t, align_bytes=64) for t in range(PACK)]
-        w1_src = w1_raw[:].rearrange("p j (b t r) -> p t b j r", t=PACK, r=RUN)
+        w1_src = w1_raw[:].rearrange("p j (b t q i) -> p t b q j i", t=PACK, q=RUN // 4, i=4)
 
-        def weave_w1(t, copy):
-            copy(out=w1_bf[t][:].rearrange("p (b r) j -> p b j r", r=RUN), in_=w1_src[:, t, :, :, :])
+        def weave_w1(t, blocks, copy):
+            copy(
+                out=w1_bf[t][:].rearrange("p (b q i) j -> p b q j i", q=RUN // 4, i=4)[:, blocks, :, :, :],
+                in_=w1_src[:, t, blocks, :, :, :],
+            )
 
         def quantize_w1(t):
             nc.vector.quantize_mx(
@@ -85,10 +90,10 @@ def tile_picked_ydcons_gelu_p_kernel(tc, x_words, x_scales, w1, w2, meas, offs, 
                 in_=w1_bf[t][:].rearrange("p m j -> p (m j)"),
             )
 
-        weave_w1(0, nc.vector.tensor_copy)
-        weave_w1(2, nc.scalar.copy)
-        weave_w1(1, nc.vector.tensor_copy)
-        weave_w1(3, nc.scalar.copy)
+        weave_w1(0, slice(0, 16), nc.vector.tensor_copy)
+        weave_w1(2, slice(0, 16), nc.scalar.copy)
+        weave_w1(1, slice(0, 16), nc.vector.tensor_copy)
+        weave_w1(3, slice(0, 16), nc.scalar.copy)
         for t in range(PACK - 1):
             quantize_w1(t)
         gather(0)
@@ -103,8 +108,6 @@ def tile_picked_ydcons_gelu_p_kernel(tc, x_words, x_scales, w1, w2, meas, offs, 
             out=w2_bf[:].rearrange("p (c i) t -> p c t i", i=4),
             in_=late[:, : PACK * N].rearrange("p (t c i) -> p c t i", t=PACK, i=4),
         )
-        meas75 = keep.tile([P, V], F32, name="meas75", align_bytes=64)
-        nc.vector.tensor_scalar_mul(out=meas75[:], in0=late[:, PACK * N :], scalar1=0.75)
         nc.vector.quantize_mx(out=w2_codes[:].bitcast(FP8X4), scales=w2_scales[:], in_=w2_bf[:].rearrange("p n j -> p (n j)"))
 
         pre = [psum.tile([P, PACK, CHUNK], F32, name="pre%d" % c) for c in range(CHUNKS)]
@@ -121,15 +124,18 @@ def tile_picked_ydcons_gelu_p_kernel(tc, x_words, x_scales, w1, w2, meas, offs, 
                 )
 
         y = keep.tile([P, S], F32, name="y", align_bytes=64)
-        for c in range(CHUNKS):
-            h_bf = keep.tile([P, CHUNK, PACK], BF16, name="h_bf%d" % c, align_bytes=64)
-            h_codes = keep.tile([P, CHUNK], U32, name="h_codes%d" % c, align_bytes=64)
-            h_scales = keep.tile([P, CHUNK], U8, name="h_scales%d" % c, align_bytes=64)
-            y_acc = psum.tile([P, CHUNK], F32, name="y_acc%d" % c)
-            nc.scalar.activation(out=h_bf[:], in_=pre[c][:].rearrange("p t n -> p n t"), func=GELU)
+        y_acc = [psum.tile([P, width], F32, name="y_acc%d" % g) for g, (first, width) in enumerate(GROUPS)]
+
+        def second_layer(first, width, g):
+            c, inside = divmod(first, CHUNK)
+            h_bf = keep.tile([P, width, PACK], BF16, name="h_bf%d" % first, align_bytes=64)
+            h_codes = keep.tile([P, width], U32, name="h_codes%d" % first, tag="h_codes%d" % first, align_bytes=64)
+            h_scales = keep.tile([P, width], U8, name="h_scales%d" % first, align_bytes=64)
+            nc.scalar.activation(out=h_bf[:], in_=pre[c][:, :, inside : inside + width].rearrange("p t n -> p n t"), func=GELU)
             nc.vector.quantize_mx(out=h_codes[:].bitcast(FP8X4), scales=h_scales[:], in_=h_bf[:].rearrange("p n t -> p (n t)"))
+            at = first - GROUPS[g][0]
             nc.tensor.matmul_mx(
-                out=y_acc[:],
+                out=y_acc[g][:, at : at + width],
                 lhsT=w2_codes[:].bitcast(FP8X4),
                 lhsT_scale=w2_scales[:],
                 rhs=h_codes[:].bitcast(FP8X4),
@@ -137,11 +143,19 @@ def tile_picked_ydcons_gelu_p_kernel(tc, x_words, x_scales, w1, w2, meas, offs, 
                 start=True,
                 stop=True,
             )
-            cols = slice(c * CHUNK, (c + 1) * CHUNK)
-            if c == CHUNKS - 1:
-                nc.scalar.copy(out=y[:, cols], in_=y_acc[:])
-            else:
-                nc.vector.tensor_copy(out=y[:, cols], in_=y_acc[:])
+
+        def group_cols(g):
+            return slice(GROUPS[g][0], GROUPS[g][0] + GROUPS[g][1])
+
+        second_layer(0, 128, 0)
+        second_layer(128, 128, 0)
+        second_layer(256, 128, 1)
+        second_layer(384, 128, 2)
+        nc.vector.tensor_copy(out=y[:, group_cols(0)], in_=y_acc[0][:])
+        for g in (1, 2):
+            nc.scalar.copy(out=y[:, group_cols(g)], in_=y_acc[g][:])
+        meas75 = keep.tile([P, V], F32, name="meas75", tag="h_codes384", align_bytes=64)
+        nc.scalar.activation(out=meas75[:], in_=late[:, PACK * N :], func=COPY, scale=0.75)
 
         picked = keep.tile([P, V], F32, name="picked", align_bytes=64)
         nc.vector.tensor_tensor(out=picked[:], in0=y[:].indirect(line_t[:]), in1=quarter[:], op=MULT)

@@ -50,8 +50,8 @@ def tile_picked_ydcons_gelu_p_kernel(tc, x_words, x_scales, w1, w2, meas, offs, 
         w1_rows = w1.rearrange("(p j) c -> p j c", j=PACK)
         nc.sync.dma_start(out=offs_t[:], in_=offs)
         nc.sync.dma_start(out=w1_raw[:, :1, :], in_=w1_rows[:, :1, :])
-        for q in range(4):
-            nc.sync.dma_start(out=xs[32 * q : 32 * q + 4, :].bitcast(I32), in_=x_scales[0][4 * q : 4 * q + 4, :].bitcast(I32))
+        for r in range(4):
+            nc.sync.dma_start(out=xs[r:P:32, :].bitcast(I32), in_=x_scales[0][r:16:4, :].bitcast(I32))
         nc.sync.dma_start(out=w1_raw[:, 1:, :], in_=w1_rows[:, 1:, :])
         nc.sync.dma_start(out=xw[:].bitcast(I32), in_=x_words[0].rearrange("p n t -> p (n t)").bitcast(I32))
 

@@ -22,6 +22,7 @@ CHUNK = 128
 CHUNKS = S // CHUNK
 BLOCK = 32
 RUN = BLOCK // PACK
+W1_FIRST = 768
 GROUPS = ((0, 256), (256, 128), (384, 128))
 COPY = mybir.ActivationFunctionType.Copy
 
@@ -36,7 +37,7 @@ def tile_picked_ydcons_gelu_p_kernel(tc, x_words, x_scales, w1, w2, meas, offs, 
         line_t = keep.tile([P, V // 16], U16, name="line_t")
         xw = keep.tile([P, T], U32, name="xw", align_bytes=64)
         xs = keep.tile([P, T], U8, name="xs", tag="chain0", align_bytes=64)
-        w1_raw = keep.tile([P, PACK, H], F32, name="w1_raw", align_bytes=64)
+        w1_raw = keep.tile([P, PACK * H], F32, name="w1_raw", align_bytes=64)
         warm = keep.tile([P, 1], F32, name="warm", tag="early_late", align_bytes=64)
         warm_out = keep.tile([P, 1], F32, name="warm_out")
 
@@ -47,12 +48,12 @@ def tile_picked_ydcons_gelu_p_kernel(tc, x_words, x_scales, w1, w2, meas, offs, 
         nc.vector.memset(quarter[:], 0.25)
 
 
-        w1_rows = w1.rearrange("(p j) c -> p j c", j=PACK)
+        w1_rows = w1.rearrange("(p j) c -> p (j c)", j=PACK)
         nc.sync.dma_start(out=offs_t[:], in_=offs)
-        nc.sync.dma_start(out=w1_raw[:, :1, :], in_=w1_rows[:, :1, :])
+        nc.sync.dma_start(out=w1_raw[:, :W1_FIRST], in_=w1_rows[:, :W1_FIRST])
         for r in range(4):
             nc.sync.dma_start(out=xs[r:P:32, :].bitcast(I32), in_=x_scales[0][r:16:4, :].bitcast(I32))
-        nc.sync.dma_start(out=w1_raw[:, 1:, :], in_=w1_rows[:, 1:, :])
+        nc.sync.dma_start(out=w1_raw[:, W1_FIRST:], in_=w1_rows[:, W1_FIRST:])
         nc.sync.dma_start(out=xw[:].bitcast(I32), in_=x_words[0].rearrange("p n t -> p (n t)").bitcast(I32))
 
         gs = keep.tile([P, S], U8, name="gs", align_bytes=64)
@@ -75,7 +76,7 @@ def tile_picked_ydcons_gelu_p_kernel(tc, x_words, x_scales, w1, w2, meas, offs, 
         w1_codes = [keep.tile([P, P], U32, name="w1_codes%d" % t, align_bytes=64) for t in range(PACK)]
         w1_scales = [keep.tile([P, P], U8, name="w1_scales%d" % t, align_bytes=64) for t in range(PACK)]
         w1_bf = [keep.tile([P, P, PACK], BF16, name="w1_bf%d" % t, tag="chain%d" % t, align_bytes=64) for t in range(PACK)]
-        w1_src = w1_raw[:].rearrange("p j (b t q i) -> p t b q j i", t=PACK, q=RUN // 4, i=4)
+        w1_src = w1_raw[:].rearrange("p (j b t q i) -> p t b q j i", j=PACK, t=PACK, q=RUN // 4, i=4)
 
         def weave_w1(t, blocks, copy):
             copy(

@@ -23,7 +23,7 @@ CHUNKS = S // CHUNK
 BLOCK = 32
 RUN = BLOCK // PACK
 W1_FIRST = 768
-GROUPS = ((0, 256), (256, 128), (384, 128))
+GROUPS = ((0, 256), (256, 128), (384, 64), (448, 64))
 COPY = mybir.ActivationFunctionType.Copy
 
 
@@ -102,7 +102,7 @@ def tile_picked_ydcons_gelu_p_kernel(tc, x_words, x_scales, w1, w2, meas, offs, 
         for c in range(1, CHUNKS):
             gather(c)
 
-        w2_bf = keep.tile([P, N, PACK], BF16, name="w2_bf", align_bytes=64)
+        w2_bf = keep.tile([P, N, PACK], BF16, name="w2_bf", tag="h_codes", align_bytes=64)
         w2_codes = keep.tile([P, N], U32, name="w2_codes", align_bytes=64)
         w2_scales = keep.tile([P, N], U8, name="w2_scales", align_bytes=64)
         nc.vector.tensor_copy(
@@ -127,19 +127,21 @@ def tile_picked_ydcons_gelu_p_kernel(tc, x_words, x_scales, w1, w2, meas, offs, 
         y = keep.tile([P, S], F32, name="y", align_bytes=64)
         y_acc = [psum.tile([P, width], F32, name="y_acc%d" % g) for g, (first, width) in enumerate(GROUPS)]
 
+        h_all = keep.tile([P, S], U32, name="h_all", tag="h_codes", align_bytes=64)
+
         def second_layer(first, width, g):
             c, inside = divmod(first, CHUNK)
             h_bf = keep.tile([P, width, PACK], BF16, name="h_bf%d" % first, align_bytes=64)
-            h_codes = keep.tile([P, width], U32, name="h_codes%d" % first, tag="h_codes%d" % first, align_bytes=64)
+            h_codes = h_all[:, first : first + width]
             h_scales = keep.tile([P, width], U8, name="h_scales%d" % first, align_bytes=64)
             nc.scalar.activation(out=h_bf[:], in_=pre[c][:, :, inside : inside + width].rearrange("p t n -> p n t"), func=GELU)
-            nc.vector.quantize_mx(out=h_codes[:].bitcast(FP8X4), scales=h_scales[:], in_=h_bf[:].rearrange("p n t -> p (n t)"))
+            nc.vector.quantize_mx(out=h_codes.bitcast(FP8X4), scales=h_scales[:], in_=h_bf[:].rearrange("p n t -> p (n t)"))
             at = first - GROUPS[g][0]
             nc.tensor.matmul_mx(
                 out=y_acc[g][:, at : at + width],
                 lhsT=w2_codes[:].bitcast(FP8X4),
                 lhsT_scale=w2_scales[:],
-                rhs=h_codes[:].bitcast(FP8X4),
+                rhs=h_codes.bitcast(FP8X4),
                 rhs_scale=h_scales[:],
                 start=True,
                 stop=True,
@@ -151,11 +153,11 @@ def tile_picked_ydcons_gelu_p_kernel(tc, x_words, x_scales, w1, w2, meas, offs, 
         second_layer(0, 128, 0)
         second_layer(128, 128, 0)
         second_layer(256, 128, 1)
-        second_layer(384, 128, 2)
-        nc.vector.tensor_copy(out=y[:, group_cols(0)], in_=y_acc[0][:])
-        for g in (1, 2):
+        second_layer(384, 64, 2)
+        second_layer(448, 64, 3)
+        for g in range(len(GROUPS)):
             nc.scalar.copy(out=y[:, group_cols(g)], in_=y_acc[g][:])
-        meas75 = keep.tile([P, V], F32, name="meas75", tag="h_codes384", align_bytes=64)
+        meas75 = keep.tile([P, V], F32, name="meas75", tag="h_codes", align_bytes=64)
         nc.scalar.activation(out=meas75[:], in_=late[:, PACK * N :], func=COPY, scale=0.75)
 
         picked = keep.tile([P, V], F32, name="picked", align_bytes=64)

@@ -46,6 +46,8 @@ def tile_picked_ydcons_gelu_p_kernel(tc, x_words, x_scales, w1, w2, meas, offs, 
         nc.scalar.activation(out=warm_out[:], in_=warm[:], func=GELU)
         quarter = keep.tile([P, V], F32, name="quarter", align_bytes=64)
         nc.vector.memset(quarter[:], 0.25)
+        h_all = keep.tile([P, S], U32, name="h_all", align_bytes=64)
+        nc.vector.memset(h_all[:].bitcast(I32), 0)
 
 
         w1_rows = w1.rearrange("(p j) c -> p (j c)", j=PACK)
@@ -58,6 +60,18 @@ def tile_picked_ydcons_gelu_p_kernel(tc, x_words, x_scales, w1, w2, meas, offs, 
 
         gs = keep.tile([P, S], U8, name="gs", align_bytes=64)
         nc.vector.tensor_copy(out=gs[:], in_=xs[:].indirect(offs_t[:]))
+
+        idle = psum.tile([P // 2, S], F32, name="idle", tag="y_acc0")
+        for n in range(2):
+            nc.tensor.matmul_mx(
+                out=idle[:],
+                lhsT=h_all[:, : P // 2].bitcast(FP8X4),
+                lhsT_scale=gs[:, : P // 2],
+                rhs=h_all[:].bitcast(FP8X4),
+                rhs_scale=gs[:],
+                start=True,
+                stop=True,
+            )
 
         late = keep.tile([P, PACK * N + V], F32, name="late", tag="early_late", align_bytes=64)
         w2_rows = w2.rearrange("(b t r) n -> t b r n", t=PACK, r=RUN)
@@ -125,24 +139,24 @@ def tile_picked_ydcons_gelu_p_kernel(tc, x_words, x_scales, w1, w2, meas, offs, 
                 )
 
         y = keep.tile([P, S], F32, name="y", align_bytes=64)
-        y_acc = [psum.tile([P, width], F32, name="y_acc%d" % g) for g, (first, width) in enumerate(GROUPS)]
+        y_acc = [psum.tile([P, width], F32, name="y_acc%d" % g, tag="y_acc%d" % g) for g, (first, width) in enumerate(GROUPS)]
 
-        h_all = keep.tile([P, S], U32, name="h_all", tag="h_codes", align_bytes=64)
+        h_scales_all = keep.tile([P, S], U8, name="h_scales_all", tag="h_codes", align_bytes=64)
 
         def second_layer(first, width, g):
             c, inside = divmod(first, CHUNK)
             h_bf = keep.tile([P, width, PACK], BF16, name="h_bf%d" % first, align_bytes=64)
             h_codes = h_all[:, first : first + width]
-            h_scales = keep.tile([P, width], U8, name="h_scales%d" % first, align_bytes=64)
+            h_scales = h_scales_all[:, first : first + width]
             nc.scalar.activation(out=h_bf[:], in_=pre[c][:, :, inside : inside + width].rearrange("p t n -> p n t"), func=GELU)
-            nc.vector.quantize_mx(out=h_codes.bitcast(FP8X4), scales=h_scales[:], in_=h_bf[:].rearrange("p n t -> p (n t)"))
+            nc.vector.quantize_mx(out=h_codes.bitcast(FP8X4), scales=h_scales, in_=h_bf[:].rearrange("p n t -> p (n t)"))
             at = first - GROUPS[g][0]
             nc.tensor.matmul_mx(
                 out=y_acc[g][:, at : at + width],
                 lhsT=w2_codes[:].bitcast(FP8X4),
                 lhsT_scale=w2_scales[:],
                 rhs=h_codes.bitcast(FP8X4),
-                rhs_scale=h_scales[:],
+                rhs_scale=h_scales,
                 start=True,
                 stop=True,
             )

@@ -13,7 +13,6 @@ U16 = mybir.dt.uint16
 U8 = mybir.dt.uint8
 FP8X4 = mybir.dt.float8_e4m3fn_x4
 GELU = mybir.ActivationFunctionType.Gelu_apprx_tanh
-MULT = mybir.AluOpType.mult
 ADD = mybir.AluOpType.add
 
 P = 128
@@ -44,9 +43,7 @@ def tile_picked_ydcons_gelu_p_kernel(tc, x_words, x_scales, w1, w2, meas, offs, 
         nc.vector.memset(xs[:].bitcast(I32), 0)
         nc.vector.memset(warm[:], 0.0)
         nc.scalar.activation(out=warm_out[:], in_=warm[:], func=GELU)
-        quarter = keep.tile([P, V], F32, name="quarter", align_bytes=64)
-        nc.vector.memset(quarter[:], 0.25)
-        h_all = keep.tile([P, S], U32, name="h_all", align_bytes=64)
+        h_all = keep.tile([P, S], U32, name="h_all", tag="h_all", align_bytes=64)
         nc.vector.memset(h_all[:].bitcast(I32), 0)
 
 
@@ -138,7 +135,7 @@ def tile_picked_ydcons_gelu_p_kernel(tc, x_words, x_scales, w1, w2, meas, offs, 
                     stop=True,
                 )
 
-        y = keep.tile([P, S], F32, name="y", align_bytes=64)
+        y_quarter = keep.tile([P, S], F32, name="y_quarter", align_bytes=64)
         y_acc = [psum.tile([P, width], F32, name="y_acc%d" % g, tag="y_acc%d" % g) for g, (first, width) in enumerate(GROUPS)]
 
         h_scales_all = keep.tile([P, S], U8, name="h_scales_all", tag="h_codes", align_bytes=64)
@@ -170,11 +167,15 @@ def tile_picked_ydcons_gelu_p_kernel(tc, x_words, x_scales, w1, w2, meas, offs, 
         second_layer(384, 64, 2)
         second_layer(448, 64, 3)
         for g in range(len(GROUPS)):
-            nc.scalar.copy(out=y[:, group_cols(g)], in_=y_acc[g][:])
-        meas75 = keep.tile([P, V], F32, name="meas75", tag="h_codes", align_bytes=64)
+            nc.scalar.activation(out=y_quarter[:, group_cols(g)], in_=y_acc[g][:], func=COPY, scale=0.25)
+        y = keep.tile([P, S], F32, name="y", tag="h_codes", align_bytes=64)
+        for g in range(len(GROUPS)):
+            copy = nc.vector.tensor_copy if g == 0 else nc.scalar.copy
+            copy(out=y[:, group_cols(g)], in_=y_acc[g][:])
+        meas75 = keep.tile([P, V], F32, name="meas75", tag="h_all", align_bytes=64)
         nc.scalar.activation(out=meas75[:], in_=late[:, PACK * N :], func=COPY, scale=0.75)
 
         picked = keep.tile([P, V], F32, name="picked", align_bytes=64)
-        nc.vector.tensor_tensor(out=picked[:], in0=y[:].indirect(line_t[:]), in1=quarter[:], op=MULT)
+        nc.vector.tensor_copy(out=picked[:], in_=y_quarter[:].indirect(line_t[:]))
         nc.vector.tensor_tensor(out=y[:].indirect(line_t[:]), in0=picked[:], in1=meas75[:], op=ADD)
         nc.sync.dma_start(out=out, in_=y[:])

@@ -122,6 +122,9 @@ def tile_picked_ydcons_gelu_p_kernel(tc, x_words, x_scales, w1, w2, meas, offs, 
         )
         nc.vector.quantize_mx(out=w2_codes[:].bitcast(FP8X4), scales=w2_scales[:], in_=w2_bf[:].rearrange("p n j -> p (n j)"))
 
+        meas75 = keep.tile([P, V], F32, name="meas75", align_bytes=64)
+        nc.vector.tensor_scalar_mul(out=meas75[:], in0=late[:, PACK * N :], scalar1=0.75)
+
         pre = [psum.tile([P, PACK, CHUNK], F32, name="pre%d" % c) for c in range(CHUNKS)]
         for c in range(CHUNKS):
             for t in range(PACK):
@@ -172,10 +175,8 @@ def tile_picked_ydcons_gelu_p_kernel(tc, x_words, x_scales, w1, w2, meas, offs, 
         for g in range(len(GROUPS)):
             copy = nc.vector.tensor_copy if g == 0 else nc.scalar.copy
             copy(out=y[:, group_cols(g)], in_=y_acc[g][:])
-        meas75 = keep.tile([P, V], F32, name="meas75", tag="h_all", align_bytes=64)
-        nc.scalar.activation(out=meas75[:], in_=late[:, PACK * N :], func=COPY, scale=0.75)
 
         picked = keep.tile([P, V], F32, name="picked", align_bytes=64)
-        nc.vector.tensor_copy(out=picked[:], in_=y_quarter[:].indirect(line_t[:]))
-        nc.vector.tensor_tensor(out=y[:].indirect(line_t[:]), in0=picked[:], in1=meas75[:], op=ADD)
+        nc.vector.tensor_tensor(out=picked[:], in0=y_quarter[:].indirect(line_t[:]), in1=meas75[:], op=ADD)
+        nc.vector.tensor_copy(out=y[:].indirect(line_t[:]), in_=picked[:])
         nc.sync.dma_start(out=out, in_=y[:])

@@ -21,7 +21,7 @@ CHUNK = 128
 CHUNKS = S // CHUNK
 BLOCK = 32
 RUN = BLOCK // PACK
-W1_FIRST = 768
+W1_FIRST = 1024
 GROUPS = ((0, 256), (256, 128), (384, 64), (448, 64))
 COPY = mybir.ActivationFunctionType.Copy
 
@@ -35,7 +35,7 @@ def tile_picked_ydcons_gelu_p_kernel(tc, x_words, x_scales, w1, w2, meas, offs, 
         offs_t = keep.tile([P, S // 16], U16, name="offs_t")
         line_t = keep.tile([P, V // 16], U16, name="line_t")
         xw = keep.tile([P, T], U32, name="xw", align_bytes=64)
-        xs = keep.tile([P, T], U8, name="xs", tag="chain0", align_bytes=64)
+        xs = keep.tile([P, T], U8, name="xs", align_bytes=64)
         w1_raw = keep.tile([P, PACK * H], F32, name="w1_raw", align_bytes=64)
         warm = keep.tile([P, 1], F32, name="warm", tag="early_late", align_bytes=64)
         warm_out = keep.tile([P, 1], F32, name="warm_out")
@@ -45,18 +45,20 @@ def tile_picked_ydcons_gelu_p_kernel(tc, x_words, x_scales, w1, w2, meas, offs, 
         nc.scalar.activation(out=warm_out[:], in_=warm[:], func=GELU)
         h_all = keep.tile([P, S], U32, name="h_all", tag="h_all", align_bytes=64)
         nc.vector.memset(h_all[:].bitcast(I32), 0)
+        gs = keep.tile([P, S], U8, name="gs", align_bytes=64)
+        nc.vector.memset(gs[:].bitcast(I32), 0)
 
 
         w1_rows = w1.rearrange("(p j) c -> p (j c)", j=PACK)
-        nc.sync.dma_start(out=offs_t[:], in_=offs)
         nc.sync.dma_start(out=w1_raw[:, :W1_FIRST], in_=w1_rows[:, :W1_FIRST])
+        nc.sync.dma_start(out=offs_t[:], in_=offs)
         for r in range(4):
             nc.sync.dma_start(out=xs[r:P:32, :].bitcast(I32), in_=x_scales[0][r:16:4, :].bitcast(I32))
         nc.sync.dma_start(out=w1_raw[:, W1_FIRST:], in_=w1_rows[:, W1_FIRST:])
         nc.sync.dma_start(out=xw[:].bitcast(I32), in_=x_words[0].rearrange("p n t -> p (n t)").bitcast(I32))
 
-        gs = keep.tile([P, S], U8, name="gs", align_bytes=64)
-        nc.vector.tensor_copy(out=gs[:], in_=xs[:].indirect(offs_t[:]))
+        early = S - CHUNK
+        nc.vector.tensor_copy(out=gs[:, :early], in_=xs[:].indirect(offs_t[:, : early // 16]))
 
         idle = psum.tile([P // 2, S], F32, name="idle", tag="y_acc0")
         for n in range(2):
@@ -89,10 +91,10 @@ def tile_picked_ydcons_gelu_p_kernel(tc, x_words, x_scales, w1, w2, meas, offs, 
         w1_bf = [keep.tile([P, P, PACK], BF16, name="w1_bf%d" % t, tag="chain%d" % t, align_bytes=64) for t in range(PACK)]
         w1_src = w1_raw[:].rearrange("p (j b t q i) -> p t b q j i", j=PACK, t=PACK, q=RUN // 4, i=4)
 
-        def weave_w1(t, blocks, copy):
+        def weave_w1(t, rows, copy):
             copy(
-                out=w1_bf[t][:].rearrange("p (b q i) j -> p b q j i", q=RUN // 4, i=4)[:, blocks, :, :, :],
-                in_=w1_src[:, t, blocks, :, :, :],
+                out=w1_bf[t][:].rearrange("p (b q i) j -> p b q j i", q=RUN // 4, i=4)[:, :, :, rows, :],
+                in_=w1_src[:, t, :, :, rows, :],
             )
 
         def quantize_w1(t):
@@ -102,11 +104,14 @@ def tile_picked_ydcons_gelu_p_kernel(tc, x_words, x_scales, w1, w2, meas, offs, 
                 in_=w1_bf[t][:].rearrange("p m j -> p (m j)"),
             )
 
-        weave_w1(0, slice(0, 16), nc.vector.tensor_copy)
-        weave_w1(2, slice(0, 16), nc.scalar.copy)
-        weave_w1(1, slice(0, 16), nc.vector.tensor_copy)
-        weave_w1(3, slice(0, 16), nc.scalar.copy)
-        for t in range(PACK - 1):
+        weave_w1(2, slice(0, 2), nc.scalar.copy)
+        weave_w1(3, slice(0, 2), nc.scalar.copy)
+        weave_w1(1, slice(0, 2), nc.vector.tensor_copy)
+        weave_w1(0, slice(0, 4), nc.vector.tensor_copy)
+        weave_w1(2, slice(2, 4), nc.scalar.copy)
+        weave_w1(1, slice(2, 4), nc.vector.tensor_copy)
+        weave_w1(3, slice(2, 4), nc.scalar.copy)
+        for t in (0, 2, 1):
             quantize_w1(t)
         gather(0)
         quantize_w1(PACK - 1)
@@ -127,13 +132,16 @@ def tile_picked_ydcons_gelu_p_kernel(tc, x_words, x_scales, w1, w2, meas, offs, 
 
         pre = [psum.tile([P, PACK, CHUNK], F32, name="pre%d" % c) for c in range(CHUNKS)]
         for c in range(CHUNKS):
+            if c == 1:
+                gs_last = keep.tile([P, CHUNK], U8, name="gs_last", tag="chain0", align_bytes=64)
+                nc.vector.tensor_copy(out=gs_last[:], in_=xs[:].indirect(offs_t[:, early // 16 :]))
             for t in range(PACK):
                 nc.tensor.matmul_mx(
                     out=pre[c][:, t, :],
                     lhsT=w1_codes[t][:].bitcast(FP8X4),
                     lhsT_scale=w1_scales[t][:],
                     rhs=gw[c][:].bitcast(FP8X4),
-                    rhs_scale=gs[:, c * CHUNK : (c + 1) * CHUNK],
+                    rhs_scale=gs[:, c * CHUNK : (c + 1) * CHUNK] if c < CHUNKS - 1 else gs_last[:],
                     start=True,
                     stop=True,
                 )

@@ -57,8 +57,16 @@ def tile_picked_ydcons_gelu_p_kernel(tc, x_words, x_scales, w1, w2, meas, offs, 
         nc.sync.dma_start(out=w1_raw[:, W1_FIRST:], in_=w1_rows[:, W1_FIRST:])
         nc.sync.dma_start(out=xw[:].bitcast(I32), in_=x_words[0].rearrange("p n t -> p (n t)").bitcast(I32))
 
-        early = S - CHUNK
+        early = 2 * CHUNK
         nc.vector.tensor_copy(out=gs[:, :early], in_=xs[:].indirect(offs_t[:, : early // 16]))
+        scale_planes = [gs[:, :CHUNK], gs[:, CHUNK:early]]
+
+        def gather_scales(c, tag):
+            plane = keep.tile([P, CHUNK], U8, name="gs%d" % c, tag=tag, align_bytes=64)
+            nc.vector.tensor_copy(out=plane[:], in_=xs[:].indirect(offs_t[:, c * CHUNK // 16 : (c + 1) * CHUNK // 16]))
+            scale_planes.append(plane[:])
+
+        gather_scales(2, "gs2")
 
         idle = psum.tile([P // 2, S], F32, name="idle", tag="y_acc0")
         for n in range(2):
@@ -133,15 +141,14 @@ def tile_picked_ydcons_gelu_p_kernel(tc, x_words, x_scales, w1, w2, meas, offs, 
         pre = [psum.tile([P, PACK, CHUNK], F32, name="pre%d" % c) for c in range(CHUNKS)]
         for c in range(CHUNKS):
             if c == 1:
-                gs_last = keep.tile([P, CHUNK], U8, name="gs_last", tag="chain0", align_bytes=64)
-                nc.vector.tensor_copy(out=gs_last[:], in_=xs[:].indirect(offs_t[:, early // 16 :]))
+                gather_scales(3, "chain0")
             for t in range(PACK):
                 nc.tensor.matmul_mx(
                     out=pre[c][:, t, :],
                     lhsT=w1_codes[t][:].bitcast(FP8X4),
                     lhsT_scale=w1_scales[t][:],
                     rhs=gw[c][:].bitcast(FP8X4),
-                    rhs_scale=gs[:, c * CHUNK : (c + 1) * CHUNK] if c < CHUNKS - 1 else gs_last[:],
+                    rhs_scale=scale_planes[c],
                     start=True,
                     stop=True,
                 )

@@ -13,17 +13,23 @@ U16 = mybir.dt.uint16
 U8 = mybir.dt.uint8
 FP8X4 = mybir.dt.float8_e4m3fn_x4
 GELU = mybir.ActivationFunctionType.Gelu_apprx_tanh
+COPY = mybir.ActivationFunctionType.Copy
 ADD = mybir.AluOpType.add
 
 P = 128
+QUADRANT = 32
 PACK = 4
-CHUNK = 128
-CHUNKS = S // CHUNK
 BLOCK = 32
 RUN = BLOCK // PACK
-W1_FIRST = 1024
-GROUPS = ((0, 256), (256, 128), (384, 64), (448, 64))
-COPY = mybir.ActivationFunctionType.Copy
+LINE_WORDS = 4
+PER_COLUMN = 16
+CHUNK = 128
+CHUNKS = S // CHUNK
+HALF = CHUNK // 2
+W1_FIRST = 2 * H
+EARLY = 2 * CHUNK
+GROUPS = ((0, 2 * CHUNK), (2 * CHUNK, CHUNK), (3 * CHUNK, HALF), (3 * CHUNK + HALF, HALF))
+VECTOR_GROUPS = 2
 
 
 def tile_picked_ydcons_gelu_p_kernel(tc, x_words, x_scales, w1, w2, meas, offs, line, out):
@@ -32,44 +38,47 @@ def tile_picked_ydcons_gelu_p_kernel(tc, x_words, x_scales, w1, w2, meas, offs, 
         keep = ctx.enter_context(tc.tile_pool(name="keep", bufs=1))
         psum = ctx.enter_context(tc.psum_pool(name="psum", bufs=1))
 
-        offs_t = keep.tile([P, S // 16], U16, name="offs_t")
-        line_t = keep.tile([P, V // 16], U16, name="line_t")
+        offs_t = keep.tile([P, S // PER_COLUMN], U16, name="offs_t")
+        line_t = keep.tile([P, V // PER_COLUMN], U16, name="line_t")
         xw = keep.tile([P, T], U32, name="xw", align_bytes=64)
         xs = keep.tile([P, T], U8, name="xs", align_bytes=64)
         w1_raw = keep.tile([P, PACK * H], F32, name="w1_raw", align_bytes=64)
         warm = keep.tile([P, 1], F32, name="warm", tag="early_late", align_bytes=64)
         warm_out = keep.tile([P, 1], F32, name="warm_out")
 
+        def offs_slice(first, count):
+            return offs_t[:, first // PER_COLUMN : (first + count) // PER_COLUMN]
+
         nc.vector.memset(xs[:].bitcast(I32), 0)
+
         nc.vector.memset(warm[:], 0.0)
         nc.scalar.activation(out=warm_out[:], in_=warm[:], func=GELU)
+
         h_all = keep.tile([P, S], U32, name="h_all", tag="h_all", align_bytes=64)
         nc.vector.memset(h_all[:].bitcast(I32), 0)
         gs = keep.tile([P, S], U8, name="gs", align_bytes=64)
         nc.vector.memset(gs[:].bitcast(I32), 0)
 
-
         w1_rows = w1.rearrange("(p j) c -> p (j c)", j=PACK)
         nc.sync.dma_start(out=w1_raw[:, :W1_FIRST], in_=w1_rows[:, :W1_FIRST])
         nc.sync.dma_start(out=offs_t[:], in_=offs)
-        for r in range(4):
-            nc.sync.dma_start(out=xs[r:P:32, :].bitcast(I32), in_=x_scales[0][r:16:4, :].bitcast(I32))
+        for r in range(PACK):
+            nc.sync.dma_start(out=xs[r:P:QUADRANT, :].bitcast(I32), in_=x_scales[0][r : K // BLOCK : PACK, :].bitcast(I32))
         nc.sync.dma_start(out=w1_raw[:, W1_FIRST:], in_=w1_rows[:, W1_FIRST:])
         nc.sync.dma_start(out=xw[:].bitcast(I32), in_=x_words[0].rearrange("p n t -> p (n t)").bitcast(I32))
 
-        early = 2 * CHUNK
-        nc.vector.tensor_copy(out=gs[:, :early], in_=xs[:].indirect(offs_t[:, : early // 16]))
-        scale_planes = [gs[:, :CHUNK], gs[:, CHUNK:early]]
+        nc.vector.tensor_copy(out=gs[:, :EARLY], in_=xs[:].indirect(offs_slice(0, EARLY)))
+        x_planes = [gs[:, :CHUNK], gs[:, CHUNK:EARLY]]
 
         def gather_scales(c, tag):
             plane = keep.tile([P, CHUNK], U8, name="gs%d" % c, tag=tag, align_bytes=64)
-            nc.vector.tensor_copy(out=plane[:], in_=xs[:].indirect(offs_t[:, c * CHUNK // 16 : (c + 1) * CHUNK // 16]))
-            scale_planes.append(plane[:])
+            nc.vector.tensor_copy(out=plane[:], in_=xs[:].indirect(offs_slice(c * CHUNK, CHUNK)))
+            x_planes.append(plane[:])
 
         gather_scales(2, "gs2")
 
         idle = psum.tile([P // 2, S], F32, name="idle", tag="y_acc0")
-        for n in range(2):
+        for warm_pass in range(2):
             nc.tensor.matmul_mx(
                 out=idle[:],
                 lhsT=h_all[:, : P // 2].bitcast(FP8X4),
@@ -90,18 +99,18 @@ def tile_picked_ydcons_gelu_p_kernel(tc, x_words, x_scales, w1, w2, meas, offs, 
         gw = []
         gw_tags = ("chain0", "chain2", "chain3", "chain1")
 
-        def gather(c):
+        def gather_words(c):
             gw.append(keep.tile([P, CHUNK], U32, name="gw%d" % c, tag=gw_tags[c], align_bytes=64))
-            nc.vector.tensor_copy(out=gw[c][:], in_=xw[:].indirect(offs_t[:, c * CHUNK // 16 : (c + 1) * CHUNK // 16]))
+            nc.vector.tensor_copy(out=gw[c][:], in_=xw[:].indirect(offs_slice(c * CHUNK, CHUNK)))
 
         w1_codes = [keep.tile([P, P], U32, name="w1_codes%d" % t, align_bytes=64) for t in range(PACK)]
         w1_scales = [keep.tile([P, P], U8, name="w1_scales%d" % t, align_bytes=64) for t in range(PACK)]
         w1_bf = [keep.tile([P, P, PACK], BF16, name="w1_bf%d" % t, tag="chain%d" % t, align_bytes=64) for t in range(PACK)]
-        w1_src = w1_raw[:].rearrange("p (j b t q i) -> p t b q j i", j=PACK, t=PACK, q=RUN // 4, i=4)
+        w1_src = w1_raw[:].rearrange("p (j b t q u) -> p t b q j u", j=PACK, t=PACK, q=RUN // LINE_WORDS, u=LINE_WORDS)
 
-        def weave_w1(t, rows, copy):
+        def round_w1(t, rows, copy):
             copy(
-                out=w1_bf[t][:].rearrange("p (b q i) j -> p b q j i", q=RUN // 4, i=4)[:, :, :, rows, :],
+                out=w1_bf[t][:].rearrange("p (b q u) j -> p b q j u", q=RUN // LINE_WORDS, u=LINE_WORDS)[:, :, :, rows, :],
                 in_=w1_src[:, t, :, :, rows, :],
             )
 
@@ -112,55 +121,59 @@ def tile_picked_ydcons_gelu_p_kernel(tc, x_words, x_scales, w1, w2, meas, offs, 
                 in_=w1_bf[t][:].rearrange("p m j -> p (m j)"),
             )
 
-        weave_w1(2, slice(0, 2), nc.scalar.copy)
-        weave_w1(3, slice(0, 2), nc.scalar.copy)
-        weave_w1(1, slice(0, 2), nc.vector.tensor_copy)
-        weave_w1(0, slice(0, 4), nc.vector.tensor_copy)
-        weave_w1(2, slice(2, 4), nc.scalar.copy)
-        weave_w1(1, slice(2, 4), nc.vector.tensor_copy)
-        weave_w1(3, slice(2, 4), nc.scalar.copy)
+        first_rows, last_rows, all_rows = slice(0, 2), slice(2, 4), slice(0, 4)
+        round_w1(2, first_rows, nc.scalar.copy)
+        round_w1(3, first_rows, nc.scalar.copy)
+        round_w1(1, first_rows, nc.vector.tensor_copy)
+        round_w1(0, all_rows, nc.vector.tensor_copy)
+        round_w1(2, last_rows, nc.scalar.copy)
+        round_w1(1, last_rows, nc.vector.tensor_copy)
+        round_w1(3, last_rows, nc.scalar.copy)
         for t in (0, 2, 1):
             quantize_w1(t)
-        gather(0)
-        quantize_w1(PACK - 1)
+        gather_words(0)
+        quantize_w1(3)
         for c in range(1, CHUNKS):
-            gather(c)
+            gather_words(c)
 
-        w2_bf = keep.tile([P, N, PACK], BF16, name="w2_bf", tag="h_codes", align_bytes=64)
+        w2_bf = keep.tile([P, N, PACK], BF16, name="w2_bf", tag="after_w2", align_bytes=64)
         w2_codes = keep.tile([P, N], U32, name="w2_codes", align_bytes=64)
         w2_scales = keep.tile([P, N], U8, name="w2_scales", align_bytes=64)
         nc.vector.tensor_copy(
-            out=w2_bf[:].rearrange("p (c i) t -> p c t i", i=4),
-            in_=late[:, : PACK * N].rearrange("p (t c i) -> p c t i", t=PACK, i=4),
+            out=w2_bf[:].rearrange("p (m u) t -> p m t u", u=LINE_WORDS),
+            in_=late[:, : PACK * N].rearrange("p (t m u) -> p m t u", t=PACK, u=LINE_WORDS),
         )
-        nc.vector.quantize_mx(out=w2_codes[:].bitcast(FP8X4), scales=w2_scales[:], in_=w2_bf[:].rearrange("p n j -> p (n j)"))
+        nc.vector.quantize_mx(out=w2_codes[:].bitcast(FP8X4), scales=w2_scales[:], in_=w2_bf[:].rearrange("p n t -> p (n t)"))
 
         meas75 = keep.tile([P, V], F32, name="meas75", align_bytes=64)
         nc.vector.tensor_scalar_mul(out=meas75[:], in0=late[:, PACK * N :], scalar1=0.75)
 
         pre = [psum.tile([P, PACK, CHUNK], F32, name="pre%d" % c) for c in range(CHUNKS)]
-        for c in range(CHUNKS):
-            if c == 1:
-                gather_scales(3, "chain0")
+
+        def first_layer(c):
             for t in range(PACK):
                 nc.tensor.matmul_mx(
                     out=pre[c][:, t, :],
                     lhsT=w1_codes[t][:].bitcast(FP8X4),
                     lhsT_scale=w1_scales[t][:],
                     rhs=gw[c][:].bitcast(FP8X4),
-                    rhs_scale=scale_planes[c],
+                    rhs_scale=x_planes[c],
                     start=True,
                     stop=True,
                 )
 
+        first_layer(0)
+        gather_scales(CHUNKS - 1, "chain0")
+        for c in range(1, CHUNKS):
+            first_layer(c)
+
         y_quarter = keep.tile([P, S], F32, name="y_quarter", align_bytes=64)
         y_acc = [psum.tile([P, width], F32, name="y_acc%d" % g, tag="y_acc%d" % g) for g, (first, width) in enumerate(GROUPS)]
-
-        h_scales_all = keep.tile([P, S], U8, name="h_scales_all", tag="h_codes", align_bytes=64)
+        h_scales_all = keep.tile([P, S], U8, name="h_scales_all", tag="after_w2", align_bytes=64)
 
         def second_layer(first, width, g):
             c, inside = divmod(first, CHUNK)
-            h_bf = keep.tile([P, width, PACK], BF16, name="h_bf%d" % first, align_bytes=64)
+            h_bf = keep.tile([P, width, PACK], BF16, name="h_bf%d" % first, tag="h_bf%d" % first, align_bytes=64)
             h_codes = h_all[:, first : first + width]
             h_scales = h_scales_all[:, first : first + width]
             nc.scalar.activation(out=h_bf[:], in_=pre[c][:, :, inside : inside + width].rearrange("p t n -> p n t"), func=GELU)
@@ -176,20 +189,16 @@ def tile_picked_ydcons_gelu_p_kernel(tc, x_words, x_scales, w1, w2, meas, offs, 
                 stop=True,
             )
 
-        def group_cols(g):
-            return slice(GROUPS[g][0], GROUPS[g][0] + GROUPS[g][1])
+        for g, (first, width) in enumerate(GROUPS):
+            for piece in range(first, first + width, CHUNK):
+                second_layer(piece, min(width, CHUNK), g)
 
-        second_layer(0, 128, 0)
-        second_layer(128, 128, 0)
-        second_layer(256, 128, 1)
-        second_layer(384, 64, 2)
-        second_layer(448, 64, 3)
-        for g in range(len(GROUPS)):
-            nc.scalar.activation(out=y_quarter[:, group_cols(g)], in_=y_acc[g][:], func=COPY, scale=0.25)
-        y = keep.tile([P, S], F32, name="y", tag="h_codes", align_bytes=64)
-        for g in range(len(GROUPS)):
-            copy = nc.vector.tensor_copy if g == 0 else nc.scalar.copy
-            copy(out=y[:, group_cols(g)], in_=y_acc[g][:])
+        for g, (first, width) in enumerate(GROUPS):
+            nc.scalar.activation(out=y_quarter[:, first : first + width], in_=y_acc[g][:], func=COPY, scale=0.25)
+        y = keep.tile([P, S], F32, name="y", tag="h_bf%d" % GROUPS[-1][0], align_bytes=64)
+        for g, (first, width) in enumerate(GROUPS):
+            copy = nc.vector.tensor_copy if g < VECTOR_GROUPS else nc.scalar.copy
+            copy(out=y[:, first : first + width], in_=y_acc[g][:])
 
         picked = keep.tile([P, V], F32, name="picked", align_bytes=64)
         nc.vector.tensor_tensor(out=picked[:], in0=y_quarter[:].indirect(line_t[:]), in1=meas75[:], op=ADD)

@@ -15,6 +15,7 @@ FP8X4 = mybir.dt.float8_e4m3fn_x4
 GELU = mybir.ActivationFunctionType.Gelu_apprx_tanh
 COPY = mybir.ActivationFunctionType.Copy
 ADD = mybir.AluOpType.add
+MULT = mybir.AluOpType.mult
 
 P = 128
 QUADRANT = 32
@@ -29,7 +30,8 @@ HALF = CHUNK // 2
 W1_FIRST = 2 * H
 EARLY = 2 * CHUNK
 GROUPS = ((0, 2 * CHUNK), (2 * CHUNK, CHUNK), (3 * CHUNK, HALF), (3 * CHUNK + HALF, HALF))
-VECTOR_GROUPS = 2
+
+VECTOR_PICKS = 96
 
 
 def tile_picked_ydcons_gelu_p_kernel(tc, x_words, x_scales, w1, w2, meas, offs, line, out):
@@ -54,10 +56,10 @@ def tile_picked_ydcons_gelu_p_kernel(tc, x_words, x_scales, w1, w2, meas, offs, 
         nc.vector.memset(warm[:], 0.0)
         nc.scalar.activation(out=warm_out[:], in_=warm[:], func=GELU)
 
+        quarter = keep.tile([P, VECTOR_PICKS], F32, name="quarter", align_bytes=64)
+        nc.vector.memset(quarter[:], 0.25)
         h_all = keep.tile([P, S], U32, name="h_all", tag="h_all", align_bytes=64)
-        nc.vector.memset(h_all[:].bitcast(I32), 0)
-        gs = keep.tile([P, S], U8, name="gs", align_bytes=64)
-        nc.vector.memset(gs[:].bitcast(I32), 0)
+        gs = keep.tile([P, EARLY], U8, name="gs", align_bytes=64)
 
         w1_rows = w1.rearrange("(p j) c -> p (j c)", j=PACK)
         nc.sync.dma_start(out=w1_raw[:, :W1_FIRST], in_=w1_rows[:, :W1_FIRST])
@@ -67,7 +69,7 @@ def tile_picked_ydcons_gelu_p_kernel(tc, x_words, x_scales, w1, w2, meas, offs, 
         nc.sync.dma_start(out=w1_raw[:, W1_FIRST:], in_=w1_rows[:, W1_FIRST:])
         nc.sync.dma_start(out=xw[:].bitcast(I32), in_=x_words[0].rearrange("p n t -> p (n t)").bitcast(I32))
 
-        nc.vector.tensor_copy(out=gs[:, :EARLY], in_=xs[:].indirect(offs_slice(0, EARLY)))
+        nc.vector.tensor_copy(out=gs[:], in_=xs[:].indirect(offs_slice(0, EARLY)))
         x_planes = [gs[:, :CHUNK], gs[:, CHUNK:EARLY]]
 
         def gather_scales(c, tag):
@@ -76,18 +78,6 @@ def tile_picked_ydcons_gelu_p_kernel(tc, x_words, x_scales, w1, w2, meas, offs, 
             x_planes.append(plane[:])
 
         gather_scales(2, "gs2")
-
-        idle = psum.tile([P // 2, S], F32, name="idle", tag="y_acc0")
-        for warm_pass in range(2):
-            nc.tensor.matmul_mx(
-                out=idle[:],
-                lhsT=h_all[:, : P // 2].bitcast(FP8X4),
-                lhsT_scale=gs[:, : P // 2],
-                rhs=h_all[:].bitcast(FP8X4),
-                rhs_scale=gs[:],
-                start=True,
-                stop=True,
-            )
 
         late = keep.tile([P, PACK * N + V], F32, name="late", tag="early_late", align_bytes=64)
         w2_rows = w2.rearrange("(b t r) n -> t b r n", t=PACK, r=RUN)
@@ -167,7 +157,6 @@ def tile_picked_ydcons_gelu_p_kernel(tc, x_words, x_scales, w1, w2, meas, offs, 
         for c in range(1, CHUNKS):
             first_layer(c)
 
-        y_quarter = keep.tile([P, S], F32, name="y_quarter", align_bytes=64)
         y_acc = [psum.tile([P, width], F32, name="y_acc%d" % g, tag="y_acc%d" % g) for g, (first, width) in enumerate(GROUPS)]
         h_scales_all = keep.tile([P, S], U8, name="h_scales_all", tag="after_w2", align_bytes=64)
 
@@ -193,14 +182,14 @@ def tile_picked_ydcons_gelu_p_kernel(tc, x_words, x_scales, w1, w2, meas, offs, 
             for piece in range(first, first + width, CHUNK):
                 second_layer(piece, min(width, CHUNK), g)
 
+        y = keep.tile([P, S], F32, name="y", align_bytes=64)
         for g, (first, width) in enumerate(GROUPS):
-            nc.scalar.activation(out=y_quarter[:, first : first + width], in_=y_acc[g][:], func=COPY, scale=0.25)
-        y = keep.tile([P, S], F32, name="y", tag="h_bf%d" % GROUPS[-1][0], align_bytes=64)
-        for g, (first, width) in enumerate(GROUPS):
-            copy = nc.vector.tensor_copy if g < VECTOR_GROUPS else nc.scalar.copy
+            copy = nc.vector.tensor_copy if g == 2 else nc.scalar.copy
             copy(out=y[:, first : first + width], in_=y_acc[g][:])
 
         picked = keep.tile([P, V], F32, name="picked", align_bytes=64)
-        nc.vector.tensor_tensor(out=picked[:], in0=y_quarter[:].indirect(line_t[:]), in1=meas75[:], op=ADD)
-        nc.vector.tensor_copy(out=y[:].indirect(line_t[:]), in_=picked[:])
+        split = VECTOR_PICKS // PER_COLUMN
+        nc.vector.tensor_tensor(out=picked[:, :VECTOR_PICKS], in0=y[:].indirect(line_t[:, :split]), in1=quarter[:], op=MULT)
+        nc.scalar.activation(out=picked[:, VECTOR_PICKS:], in_=y[:].indirect(line_t[:, split:]), func=COPY, scale=0.25)
+        nc.vector.tensor_tensor(out=y[:].indirect(line_t[:]), in0=picked[:], in1=meas75[:], op=ADD)
         nc.sync.dma_start(out=out, in_=y[:])

@@ -62,7 +62,7 @@ def tile_picked_ydcons_gelu_p_kernel(tc, x_words, x_scales, w1, w2, meas, offs, 
         gs = keep.tile([P, EARLY], U8, name="gs", align_bytes=64)
 
         w1_rows = w1.rearrange("(p j) c -> p (j c)", j=PACK)
-        nc.sync.dma_start(out=w1_raw[:, :W1_FIRST], in_=w1_rows[:, :W1_FIRST])
+        nc.scalar.dma_start(out=w1_raw[:, :W1_FIRST], in_=w1_rows[:, :W1_FIRST])
         nc.sync.dma_start(out=offs_t[:], in_=offs)
         for r in range(PACK):
             nc.sync.dma_start(out=xs[r:P:QUADRANT, :].bitcast(I32), in_=x_scales[0][r : K // BLOCK : PACK, :].bitcast(I32))
@@ -111,11 +111,12 @@ def tile_picked_ydcons_gelu_p_kernel(tc, x_words, x_scales, w1, w2, meas, offs, 
                 in_=w1_bf[t][:].rearrange("p m j -> p (m j)"),
             )
 
-        first_rows, last_rows, all_rows = slice(0, 2), slice(2, 4), slice(0, 4)
+        first_rows, last_rows = slice(0, 2), slice(2, 4)
         round_w1(2, first_rows, nc.scalar.copy)
         round_w1(3, first_rows, nc.scalar.copy)
         round_w1(1, first_rows, nc.vector.tensor_copy)
-        round_w1(0, all_rows, nc.vector.tensor_copy)
+        round_w1(0, first_rows, nc.vector.tensor_copy)
+        round_w1(0, last_rows, nc.vector.tensor_copy)
         round_w1(2, last_rows, nc.scalar.copy)
         round_w1(1, last_rows, nc.vector.tensor_copy)
         round_w1(3, last_rows, nc.scalar.copy)

@@ -62,7 +62,7 @@ def tile_picked_ydcons_gelu_p_kernel(tc, x_words, x_scales, w1, w2, meas, offs, 
         gs = keep.tile([P, EARLY], U8, name="gs", align_bytes=64)
 
         w1_rows = w1.rearrange("(p j) c -> p (j c)", j=PACK)
-        nc.scalar.dma_start(out=w1_raw[:, :W1_FIRST], in_=w1_rows[:, :W1_FIRST])
+        nc.sync.dma_start(out=w1_raw[:, :W1_FIRST], in_=w1_rows[:, :W1_FIRST])
         nc.sync.dma_start(out=offs_t[:], in_=offs)
         for r in range(PACK):
             nc.sync.dma_start(out=xs[r:P:QUADRANT, :].bitcast(I32), in_=x_scales[0][r : K // BLOCK : PACK, :].bitcast(I32))
@@ -98,10 +98,10 @@ def tile_picked_ydcons_gelu_p_kernel(tc, x_words, x_scales, w1, w2, meas, offs, 
         w1_bf = [keep.tile([P, P, PACK], BF16, name="w1_bf%d" % t, tag="chain%d" % t, align_bytes=64) for t in range(PACK)]
         w1_src = w1_raw[:].rearrange("p (j b t q u) -> p t b q j u", j=PACK, t=PACK, q=RUN // LINE_WORDS, u=LINE_WORDS)
 
-        def round_w1(t, rows, copy):
+        def round_w1(t, rows, copy, blocks=slice(0, H // BLOCK)):
             copy(
-                out=w1_bf[t][:].rearrange("p (b q u) j -> p b q j u", q=RUN // LINE_WORDS, u=LINE_WORDS)[:, :, :, rows, :],
-                in_=w1_src[:, t, :, :, rows, :],
+                out=w1_bf[t][:].rearrange("p (b q u) j -> p b q j u", q=RUN // LINE_WORDS, u=LINE_WORDS)[:, blocks, :, rows, :],
+                in_=w1_src[:, t, blocks, :, rows, :],
             )
 
         def quantize_w1(t):
@@ -119,7 +119,8 @@ def tile_picked_ydcons_gelu_p_kernel(tc, x_words, x_scales, w1, w2, meas, offs, 
         round_w1(0, last_rows, nc.vector.tensor_copy)
         round_w1(2, last_rows, nc.scalar.copy)
         round_w1(1, last_rows, nc.vector.tensor_copy)
-        round_w1(3, last_rows, nc.scalar.copy)
+        round_w1(3, last_rows, nc.scalar.copy, slice(0, 8))
+        round_w1(3, last_rows, nc.vector.tensor_copy, slice(8, 16))
         for t in (0, 2, 1):
             quantize_w1(t)
         gather_words(0)

@@ -44,8 +44,8 @@ def tile_picked_ydcons_gelu_p_kernel(tc, x_words, x_scales, w1, w2, meas, offs, 
         line_t = keep.tile([P, V // PER_COLUMN], U16, name="line_t")
         xw = keep.tile([P, T], U32, name="xw", align_bytes=64)
         xs = keep.tile([P, T], U8, name="xs", align_bytes=64)
-        w1_raw = keep.tile([P, PACK * H], F32, name="w1_raw", align_bytes=64)
-        warm = keep.tile([P, 1], F32, name="warm", tag="early_late", align_bytes=64)
+        w1_raw = keep.tile([P, PACK * H], F32, name="w1_raw", tag="w1_then_late", align_bytes=64)
+        warm = keep.tile([P, 1], F32, name="warm", align_bytes=64)
         warm_out = keep.tile([P, 1], F32, name="warm_out")
 
         def offs_slice(first, count):
@@ -79,7 +79,7 @@ def tile_picked_ydcons_gelu_p_kernel(tc, x_words, x_scales, w1, w2, meas, offs, 
 
         gather_scales(2, "gs2")
 
-        late = keep.tile([P, PACK * N + V], F32, name="late", tag="early_late", align_bytes=64)
+        late = keep.tile([P, PACK * N + V], F32, name="late", tag="w1_then_late", align_bytes=64)
         w2_rows = w2.rearrange("(b t r) n -> t b r n", t=PACK, r=RUN)
         for t in range(PACK):
             nc.sync.dma_start(out=late[:, t * N : (t + 1) * N], in_=w2_rows[t])

@@ -45,16 +45,11 @@ def tile_picked_ydcons_gelu_p_kernel(tc, x_words, x_scales, w1, w2, meas, offs, 
         xw = keep.tile([P, T], U32, name="xw", align_bytes=64)
         xs = keep.tile([P, T], U8, name="xs", align_bytes=64)
         w1_raw = keep.tile([P, PACK * H], F32, name="w1_raw", tag="w1_then_late", align_bytes=64)
-        warm = keep.tile([P, 1], F32, name="warm", align_bytes=64)
-        warm_out = keep.tile([P, 1], F32, name="warm_out")
 
         def offs_slice(first, count):
             return offs_t[:, first // PER_COLUMN : (first + count) // PER_COLUMN]
 
         nc.vector.memset(xs[:].bitcast(I32), 0)
-
-        nc.vector.memset(warm[:], 0.0)
-        nc.scalar.activation(out=warm_out[:], in_=warm[:], func=GELU)
 
         quarter = keep.tile([P, VECTOR_PICKS], F32, name="quarter", align_bytes=64)
         nc.vector.memset(quarter[:], 0.25)

@@ -22,15 +22,13 @@ QUADRANT = 32
 PACK = 4
 BLOCK = 32
 RUN = BLOCK // PACK
+SCALE_ROWS = K // BLOCK
 LINE_WORDS = 4
 PER_COLUMN = 16
 CHUNK = 128
 CHUNKS = S // CHUNK
 HALF = CHUNK // 2
-W1_FIRST = 2 * H
-EARLY = 2 * CHUNK
 GROUPS = ((0, 2 * CHUNK), (2 * CHUNK, CHUNK), (3 * CHUNK, HALF), (3 * CHUNK + HALF, HALF))
-
 VECTOR_PICKS = 96
 
 
@@ -44,40 +42,40 @@ def tile_picked_ydcons_gelu_p_kernel(tc, x_words, x_scales, w1, w2, meas, offs, 
         line_t = keep.tile([P, V // PER_COLUMN], U16, name="line_t")
         xw = keep.tile([P, T], U32, name="xw", align_bytes=64)
         xs = keep.tile([P, T], U8, name="xs", align_bytes=64)
+        gs = keep.tile([P, S], U8, name="gs", align_bytes=64)
+        x_plane = keep.tile([P, S], U8, name="x_plane", align_bytes=64)
         w1_raw = keep.tile([P, PACK * H], F32, name="w1_raw", tag="w1_then_late", align_bytes=64)
 
         def offs_slice(first, count):
             return offs_t[:, first // PER_COLUMN : (first + count) // PER_COLUMN]
 
-        nc.vector.memset(xs[:].bitcast(I32), 0)
-
+        rows_at = P - SCALE_ROWS
+        nc.vector.memset(xs[:rows_at, :].bitcast(I32), 0)
+        nc.vector.memset(x_plane[:].bitcast(I32), 0)
         quarter = keep.tile([P, VECTOR_PICKS], F32, name="quarter", align_bytes=64)
         nc.vector.memset(quarter[:], 0.25)
-        h_all = keep.tile([P, S], U32, name="h_all", tag="h_all", align_bytes=64)
-        gs = keep.tile([P, EARLY], U8, name="gs", align_bytes=64)
+
+        warm = keep.tile([P, 1], F32, name="warm")
+        nc.scalar.activation(out=warm[:], in_=quarter[:, :1], func=GELU)
 
         w1_rows = w1.rearrange("(p j) c -> p (j c)", j=PACK)
-        nc.sync.dma_start(out=w1_raw[:, :W1_FIRST], in_=w1_rows[:, :W1_FIRST])
         nc.sync.dma_start(out=offs_t[:], in_=offs)
-        for r in range(PACK):
-            nc.sync.dma_start(out=xs[r:P:QUADRANT, :].bitcast(I32), in_=x_scales[0][r : K // BLOCK : PACK, :].bitcast(I32))
-        nc.sync.dma_start(out=w1_raw[:, W1_FIRST:], in_=w1_rows[:, W1_FIRST:])
+        nc.scalar.dma_start(out=xs[rows_at:, :].bitcast(I32), in_=x_scales[0].bitcast(I32))
+        nc.sync.dma_start(out=w1_raw[:, : 2 * H], in_=w1_rows[:, : 2 * H])
+        nc.sync.dma_start(out=w1_raw[:, 2 * H :], in_=w1_rows[:, 2 * H :])
         nc.sync.dma_start(out=xw[:].bitcast(I32), in_=x_words[0].rearrange("p n t -> p (n t)").bitcast(I32))
 
-        nc.vector.tensor_copy(out=gs[:], in_=xs[:].indirect(offs_slice(0, EARLY)))
-        x_planes = [gs[:, :CHUNK], gs[:, CHUNK:EARLY]]
-
-        def gather_scales(c, tag):
-            plane = keep.tile([P, CHUNK], U8, name="gs%d" % c, tag=tag, align_bytes=64)
-            nc.vector.tensor_copy(out=plane[:], in_=xs[:].indirect(offs_slice(c * CHUNK, CHUNK)))
-            x_planes.append(plane[:])
-
-        gather_scales(2, "gs2")
+        nc.vector.tensor_copy(out=gs[:], in_=xs[:].indirect(offs_t[:]))
+        for q in range(P // QUADRANT):
+            nc.sync.dma_start(
+                out=x_plane[q * QUADRANT : q * QUADRANT + PACK, :].bitcast(I32),
+                in_=gs[rows_at + q * PACK : rows_at + (q + 1) * PACK, :].bitcast(I32),
+            )
 
         late = keep.tile([P, PACK * N + V], F32, name="late", tag="w1_then_late", align_bytes=64)
-        w2_rows = w2.rearrange("(b t r) n -> t b r n", t=PACK, r=RUN)
-        for t in range(PACK):
-            nc.sync.dma_start(out=late[:, t * N : (t + 1) * N], in_=w2_rows[t])
+        w2_rows = w2.rearrange("(b g r e) n -> g b r (e n)", g=2, r=RUN, e=2)
+        for g in range(2):
+            nc.sync.dma_start(out=late[:, 2 * g * N : 2 * (g + 1) * N], in_=w2_rows[g])
         nc.sync.dma_start(out=late[:, PACK * N :], in_=meas)
         nc.sync.dma_start(out=line_t[:], in_=line)
 
@@ -91,12 +89,12 @@ def tile_picked_ydcons_gelu_p_kernel(tc, x_words, x_scales, w1, w2, meas, offs, 
         w1_codes = [keep.tile([P, P], U32, name="w1_codes%d" % t, align_bytes=64) for t in range(PACK)]
         w1_scales = [keep.tile([P, P], U8, name="w1_scales%d" % t, align_bytes=64) for t in range(PACK)]
         w1_bf = [keep.tile([P, P, PACK], BF16, name="w1_bf%d" % t, tag="chain%d" % t, align_bytes=64) for t in range(PACK)]
-        w1_src = w1_raw[:].rearrange("p (j b t q u) -> p t b q j u", j=PACK, t=PACK, q=RUN // LINE_WORDS, u=LINE_WORDS)
+        w1_src = w1_raw[:].rearrange("p (j b g q r e) -> p g e b q j r", j=PACK, g=2, q=4, r=2, e=2)
 
         def round_w1(t, rows, copy, blocks=slice(0, H // BLOCK)):
             copy(
-                out=w1_bf[t][:].rearrange("p (b q u) j -> p b q j u", q=RUN // LINE_WORDS, u=LINE_WORDS)[:, blocks, :, rows, :],
-                in_=w1_src[:, t, blocks, :, rows, :],
+                out=w1_bf[t][:].rearrange("p (b q r) j -> p b q j r", q=4, r=2)[:, blocks, :, rows, :],
+                in_=w1_src[:, t // 2, t % 2, blocks, :, rows, :],
             )
 
         def quantize_w1(t):
@@ -116,11 +114,9 @@ def tile_picked_ydcons_gelu_p_kernel(tc, x_words, x_scales, w1, w2, meas, offs, 
         round_w1(1, last_rows, nc.vector.tensor_copy)
         round_w1(3, last_rows, nc.scalar.copy, slice(0, 8))
         round_w1(3, last_rows, nc.vector.tensor_copy, slice(8, 16))
-        for t in (0, 2, 1):
+        for t in (0, 2, 1, 3):
             quantize_w1(t)
-        gather_words(0)
-        quantize_w1(3)
-        for c in range(1, CHUNKS):
+        for c in range(CHUNKS):
             gather_words(c)
 
         w2_bf = keep.tile([P, N, PACK], BF16, name="w2_bf", tag="after_w2", align_bytes=64)
@@ -136,48 +132,44 @@ def tile_picked_ydcons_gelu_p_kernel(tc, x_words, x_scales, w1, w2, meas, offs, 
         nc.vector.tensor_scalar_mul(out=meas75[:], in0=late[:, PACK * N :], scalar1=0.75)
 
         pre = [psum.tile([P, PACK, CHUNK], F32, name="pre%d" % c) for c in range(CHUNKS)]
-
-        def first_layer(c):
+        for c in range(CHUNKS):
             for t in range(PACK):
                 nc.tensor.matmul_mx(
                     out=pre[c][:, t, :],
                     lhsT=w1_codes[t][:].bitcast(FP8X4),
                     lhsT_scale=w1_scales[t][:],
                     rhs=gw[c][:].bitcast(FP8X4),
-                    rhs_scale=x_planes[c],
+                    rhs_scale=x_plane[:, c * CHUNK : (c + 1) * CHUNK],
                     start=True,
                     stop=True,
                 )
 
-        first_layer(0)
-        gather_scales(CHUNKS - 1, "chain0")
-        for c in range(1, CHUNKS):
-            first_layer(c)
-
         y_acc = [psum.tile([P, width], F32, name="y_acc%d" % g, tag="y_acc%d" % g) for g, (first, width) in enumerate(GROUPS)]
+        h_all = keep.tile([P, S], U32, name="h_all", align_bytes=64)
         h_scales_all = keep.tile([P, S], U8, name="h_scales_all", tag="after_w2", align_bytes=64)
 
-        def second_layer(first, width, g):
+        def hidden(first, width):
             c, inside = divmod(first, CHUNK)
             h_bf = keep.tile([P, width, PACK], BF16, name="h_bf%d" % first, tag="h_bf%d" % first, align_bytes=64)
-            h_codes = h_all[:, first : first + width]
-            h_scales = h_scales_all[:, first : first + width]
             nc.scalar.activation(out=h_bf[:], in_=pre[c][:, :, inside : inside + width].rearrange("p t n -> p n t"), func=GELU)
-            nc.vector.quantize_mx(out=h_codes.bitcast(FP8X4), scales=h_scales, in_=h_bf[:].rearrange("p n t -> p (n t)"))
-            at = first - GROUPS[g][0]
-            nc.tensor.matmul_mx(
-                out=y_acc[g][:, at : at + width],
-                lhsT=w2_codes[:].bitcast(FP8X4),
-                lhsT_scale=w2_scales[:],
-                rhs=h_codes.bitcast(FP8X4),
-                rhs_scale=h_scales,
-                start=True,
-                stop=True,
+            nc.vector.quantize_mx(
+                out=h_all[:, first : first + width].bitcast(FP8X4),
+                scales=h_scales_all[:, first : first + width],
+                in_=h_bf[:].rearrange("p n t -> p (n t)"),
             )
 
         for g, (first, width) in enumerate(GROUPS):
             for piece in range(first, first + width, CHUNK):
-                second_layer(piece, min(width, CHUNK), g)
+                hidden(piece, min(width, CHUNK))
+            nc.tensor.matmul_mx(
+                out=y_acc[g][:],
+                lhsT=w2_codes[:].bitcast(FP8X4),
+                lhsT_scale=w2_scales[:],
+                rhs=h_all[:, first : first + width].bitcast(FP8X4),
+                rhs_scale=h_scales_all[:, first : first + width],
+                start=True,
+                stop=True,
+            )
 
         y = keep.tile([P, S], F32, name="y", align_bytes=64)
         for g, (first, width) in enumerate(GROUPS):

@@ -29,6 +29,8 @@ CHUNK = 128
 CHUNKS = S // CHUNK
 HALF = CHUNK // 2
 GROUPS = ((0, 2 * CHUNK), (2 * CHUNK, CHUNK), (3 * CHUNK, HALF), (3 * CHUNK + HALF, HALF))
+PAIRED = 2
+WARM_ROWS, WARM_PASSES = 32, 5
 VECTOR_PICKS = 96
 
 
@@ -41,10 +43,10 @@ def tile_picked_ydcons_gelu_p_kernel(tc, x_words, x_scales, w1, w2, meas, offs, 
         offs_t = keep.tile([P, S // PER_COLUMN], U16, name="offs_t")
         line_t = keep.tile([P, V // PER_COLUMN], U16, name="line_t")
         xw = keep.tile([P, T], U32, name="xw", align_bytes=64)
-        xs = keep.tile([P, T], U8, name="xs", align_bytes=64)
+        xs = keep.tile([P, T], U8, name="xs", tag="xs_then_late", align_bytes=64)
         gs = keep.tile([P, S], U8, name="gs", align_bytes=64)
         x_plane = keep.tile([P, S], U8, name="x_plane", align_bytes=64)
-        w1_raw = keep.tile([P, PACK * H], F32, name="w1_raw", tag="w1_then_late", align_bytes=64)
+        w1_raw = keep.tile([P, PACK * H], F32, name="w1_raw", align_bytes=64)
 
         def offs_slice(first, count):
             return offs_t[:, first // PER_COLUMN : (first + count) // PER_COLUMN]
@@ -72,7 +74,7 @@ def tile_picked_ydcons_gelu_p_kernel(tc, x_words, x_scales, w1, w2, meas, offs, 
                 in_=gs[rows_at + q * PACK : rows_at + (q + 1) * PACK, :].bitcast(I32),
             )
 
-        late = keep.tile([P, PACK * N + V], F32, name="late", tag="w1_then_late", align_bytes=64)
+        late = keep.tile([P, PACK * N + V], F32, name="late", tag="xs_then_late", align_bytes=64)
         w2_rows = w2.rearrange("(b g r e) n -> g b r (e n)", g=2, r=RUN, e=2)
         for g in range(2):
             nc.sync.dma_start(out=late[:, 2 * g * N : 2 * (g + 1) * N], in_=w2_rows[g])
@@ -131,11 +133,26 @@ def tile_picked_ydcons_gelu_p_kernel(tc, x_words, x_scales, w1, w2, meas, offs, 
         meas75 = keep.tile([P, V], F32, name="meas75", align_bytes=64)
         nc.vector.tensor_scalar_mul(out=meas75[:], in0=late[:, PACK * N :], scalar1=0.75)
 
-        pre = [psum.tile([P, PACK, CHUNK], F32, name="pre%d" % c) for c in range(CHUNKS)]
+        idle = psum.tile([WARM_ROWS, CHUNK], F32, name="idle")
+        for i in range(WARM_PASSES):
+            nc.tensor.matmul_mx(
+                out=idle[:],
+                lhsT=w1_codes[0][:, :WARM_ROWS].bitcast(FP8X4),
+                lhsT_scale=w1_scales[0][:, :WARM_ROWS],
+                rhs=w1_codes[0][:].bitcast(FP8X4),
+                rhs_scale=w1_scales[0][:],
+                start=True,
+                stop=True,
+            )
+        pre = []
         for c in range(CHUNKS):
+            if c < PAIRED:
+                pre.append([psum.tile([P, 2, CHUNK], F32, name="pre%d_%d" % (c, g), tag="pre%d_%d" % (c, g)) for g in range(2)])
+            else:
+                pre.append(psum.tile([P, PACK, CHUNK], F32, name="pre%d" % c))
             for t in range(PACK):
                 nc.tensor.matmul_mx(
-                    out=pre[c][:, t, :],
+                    out=pre[c][t // 2][:, t % 2, :] if c < PAIRED else pre[c][:, t, :],
                     lhsT=w1_codes[t][:].bitcast(FP8X4),
                     lhsT_scale=w1_scales[t][:],
                     rhs=gw[c][:].bitcast(FP8X4),
@@ -144,14 +161,23 @@ def tile_picked_ydcons_gelu_p_kernel(tc, x_words, x_scales, w1, w2, meas, offs, 
                     stop=True,
                 )
 
-        y_acc = [psum.tile([P, width], F32, name="y_acc%d" % g, tag="y_acc%d" % g) for g, (first, width) in enumerate(GROUPS)]
+        y_acc = [psum.tile([P, width], F32, name="y_acc%d" % g, tag="pre%d_%d" % divmod(g, 2)) for g, (first, width) in enumerate(GROUPS)]
         h_all = keep.tile([P, S], U32, name="h_all", align_bytes=64)
         h_scales_all = keep.tile([P, S], U8, name="h_scales_all", tag="after_w2", align_bytes=64)
 
         def hidden(first, width):
             c, inside = divmod(first, CHUNK)
             h_bf = keep.tile([P, width, PACK], BF16, name="h_bf%d" % first, tag="h_bf%d" % first, align_bytes=64)
-            nc.scalar.activation(out=h_bf[:], in_=pre[c][:, :, inside : inside + width].rearrange("p t n -> p n t"), func=GELU)
+            if c < PAIRED:
+                pairs = keep.tile([P, 2, width, 2], BF16, name="pairs%d" % c, align_bytes=64)
+                for g in range(2):
+                    nc.scalar.activation(out=pairs[:, g], in_=pre[c][g][:].rearrange("p e n -> p n e"), func=GELU)
+                nc.vector.tensor_copy(
+                    out=h_bf[:].rearrange("p n t -> p (n t)").bitcast(F32).rearrange("p (m u g) -> p m g u", g=2, u=2),
+                    in_=pairs[:].rearrange("p g n e -> p (g n e)").bitcast(F32).rearrange("p (g m u) -> p m g u", g=2, u=2),
+                )
+            else:
+                nc.scalar.activation(out=h_bf[:], in_=pre[c][:, :, inside : inside + width].rearrange("p t n -> p n t"), func=GELU)
             nc.vector.quantize_mx(
                 out=h_all[:, first : first + width].bitcast(FP8X4),
                 scales=h_scales_all[:, first : first + width],

@@ -43,10 +43,10 @@ def tile_picked_ydcons_gelu_p_kernel(tc, x_words, x_scales, w1, w2, meas, offs, 
         offs_t = keep.tile([P, S // PER_COLUMN], U16, name="offs_t")
         line_t = keep.tile([P, V // PER_COLUMN], U16, name="line_t")
         xw = keep.tile([P, T], U32, name="xw", align_bytes=64)
-        xs = keep.tile([P, T], U8, name="xs", tag="xs_then_late", align_bytes=64)
+        xs = keep.tile([P, T], U8, name="xs", align_bytes=64)
         gs = keep.tile([P, S], U8, name="gs", align_bytes=64)
         x_plane = keep.tile([P, S], U8, name="x_plane", align_bytes=64)
-        w1_raw = keep.tile([P, PACK * H], F32, name="w1_raw", align_bytes=64)
+        w1_raw = keep.tile([P, PACK * H], F32, name="w1_raw", tag="w1_then_late", align_bytes=64)
 
         def offs_slice(first, count):
             return offs_t[:, first // PER_COLUMN : (first + count) // PER_COLUMN]
@@ -74,7 +74,7 @@ def tile_picked_ydcons_gelu_p_kernel(tc, x_words, x_scales, w1, w2, meas, offs, 
                 in_=gs[rows_at + q * PACK : rows_at + (q + 1) * PACK, :].bitcast(I32),
             )
 
-        late = keep.tile([P, PACK * N + V], F32, name="late", tag="xs_then_late", align_bytes=64)
+        late = keep.tile([P, PACK * N + V], F32, name="late", tag="w1_then_late", align_bytes=64)
         w2_rows = w2.rearrange("(b g r e) n -> g b r (e n)", g=2, r=RUN, e=2)
         for g in range(2):
             nc.sync.dma_start(out=late[:, 2 * g * N : 2 * (g + 1) * N], in_=w2_rows[g])

@@ -62,8 +62,9 @@ def tile_picked_ydcons_gelu_p_kernel(tc, x_words, x_scales, w1, w2, meas, offs, 
 
         w1_rows = w1.rearrange("(p j) c -> p (j c)", j=PACK)
         nc.sync.dma_start(out=offs_t[:], in_=offs)
-        nc.scalar.dma_start(out=xs[rows_at:, :].bitcast(I32), in_=x_scales[0].bitcast(I32))
-        nc.sync.dma_start(out=w1_raw[:, : 2 * H], in_=w1_rows[:, : 2 * H])
+        nc.scalar.dma_start(out=w1_raw[:, :H], in_=w1_rows[:, :H])
+        nc.sync.dma_start(out=xs[rows_at:, :].bitcast(I32), in_=x_scales[0].bitcast(I32))
+        nc.sync.dma_start(out=w1_raw[:, H : 2 * H], in_=w1_rows[:, H : 2 * H])
         nc.sync.dma_start(out=w1_raw[:, 2 * H :], in_=w1_rows[:, 2 * H :])
         nc.sync.dma_start(out=xw[:].bitcast(I32), in_=x_words[0].rearrange("p n t -> p (n t)").bitcast(I32))
 
@@ -121,7 +122,7 @@ def tile_picked_ydcons_gelu_p_kernel(tc, x_words, x_scales, w1, w2, meas, offs, 
         for c in range(CHUNKS):
             gather_words(c)
 
-        w2_bf = keep.tile([P, N, PACK], BF16, name="w2_bf", tag="after_w2", align_bytes=64)
+        w2_bf = keep.tile([P, N, PACK], BF16, name="w2_bf", align_bytes=64)
         w2_codes = keep.tile([P, N], U32, name="w2_codes", align_bytes=64)
         w2_scales = keep.tile([P, N], U8, name="w2_scales", align_bytes=64)
         nc.vector.tensor_copy(
@@ -129,9 +130,6 @@ def tile_picked_ydcons_gelu_p_kernel(tc, x_words, x_scales, w1, w2, meas, offs, 
             in_=late[:, : PACK * N].rearrange("p (t m u) -> p m t u", t=PACK, u=LINE_WORDS),
         )
         nc.vector.quantize_mx(out=w2_codes[:].bitcast(FP8X4), scales=w2_scales[:], in_=w2_bf[:].rearrange("p n t -> p (n t)"))
-
-        meas75 = keep.tile([P, V], F32, name="meas75", align_bytes=64)
-        nc.vector.tensor_scalar_mul(out=meas75[:], in0=late[:, PACK * N :], scalar1=0.75)
 
         idle = psum.tile([WARM_ROWS, CHUNK], F32, name="idle")
         for i in range(WARM_PASSES):
@@ -163,7 +161,7 @@ def tile_picked_ydcons_gelu_p_kernel(tc, x_words, x_scales, w1, w2, meas, offs, 
 
         y_acc = [psum.tile([P, width], F32, name="y_acc%d" % g, tag="pre%d_%d" % divmod(g, 2)) for g, (first, width) in enumerate(GROUPS)]
         h_all = keep.tile([P, S], U32, name="h_all", align_bytes=64)
-        h_scales_all = keep.tile([P, S], U8, name="h_scales_all", tag="after_w2", align_bytes=64)
+        h_scales_all = keep.tile([P, S], U8, name="h_scales_all", align_bytes=64)
 
         def hidden(first, width):
             c, inside = divmod(first, CHUNK)
@@ -196,6 +194,9 @@ def tile_picked_ydcons_gelu_p_kernel(tc, x_words, x_scales, w1, w2, meas, offs, 
                 start=True,
                 stop=True,
             )
+
+        meas75 = keep.tile([P, V], F32, name="meas75", tag="h_bf%d" % (S - HALF), align_bytes=64)
+        nc.vector.tensor_scalar_mul(out=meas75[:], in0=late[:, PACK * N :], scalar1=0.75)
 
         y = keep.tile([P, S], F32, name="y", align_bytes=64)
         for g, (first, width) in enumerate(GROUPS):

@@ -46,7 +46,7 @@ def tile_picked_ydcons_gelu_p_kernel(tc, x_words, x_scales, w1, w2, meas, offs, 
         xs = keep.tile([P, T], U8, name="xs", align_bytes=64)
         gs = keep.tile([P, S], U8, name="gs", align_bytes=64)
         x_plane = keep.tile([P, S], U8, name="x_plane", align_bytes=64)
-        w1_raw = keep.tile([P, PACK * H], F32, name="w1_raw", tag="w1_then_late", align_bytes=64)
+        w1_raw = [keep.tile([P, 2 * H], F32, name="w1_raw%d" % i, tag="w1_raw%d" % i, align_bytes=64) for i in range(2)]
 
         def offs_slice(first, count):
             return offs_t[:, first // PER_COLUMN : (first + count) // PER_COLUMN]
@@ -62,10 +62,10 @@ def tile_picked_ydcons_gelu_p_kernel(tc, x_words, x_scales, w1, w2, meas, offs, 
 
         w1_rows = w1.rearrange("(p j) c -> p (j c)", j=PACK)
         nc.sync.dma_start(out=offs_t[:], in_=offs)
-        nc.scalar.dma_start(out=w1_raw[:, :H], in_=w1_rows[:, :H])
+        nc.scalar.dma_start(out=w1_raw[0][:, :H], in_=w1_rows[:, :H])
         nc.sync.dma_start(out=xs[rows_at:, :].bitcast(I32), in_=x_scales[0].bitcast(I32))
-        nc.sync.dma_start(out=w1_raw[:, H : 2 * H], in_=w1_rows[:, H : 2 * H])
-        nc.sync.dma_start(out=w1_raw[:, 2 * H :], in_=w1_rows[:, 2 * H :])
+        nc.sync.dma_start(out=w1_raw[0][:, H:], in_=w1_rows[:, H : 2 * H])
+        nc.sync.dma_start(out=w1_raw[1][:], in_=w1_rows[:, 2 * H :])
         nc.sync.dma_start(out=xw[:].bitcast(I32), in_=x_words[0].rearrange("p n t -> p (n t)").bitcast(I32))
 
         nc.vector.tensor_copy(out=gs[:], in_=xs[:].indirect(offs_t[:]))
@@ -75,12 +75,6 @@ def tile_picked_ydcons_gelu_p_kernel(tc, x_words, x_scales, w1, w2, meas, offs, 
                 in_=gs[rows_at + q * PACK : rows_at + (q + 1) * PACK, :].bitcast(I32),
             )
 
-        late = keep.tile([P, PACK * N + V], F32, name="late", tag="w1_then_late", align_bytes=64)
-        w2_rows = w2.rearrange("(b g r e) n -> g b r (e n)", g=2, r=RUN, e=2)
-        for g in range(2):
-            nc.sync.dma_start(out=late[:, 2 * g * N : 2 * (g + 1) * N], in_=w2_rows[g])
-        nc.sync.dma_start(out=late[:, PACK * N :], in_=meas)
-        nc.sync.dma_start(out=line_t[:], in_=line)
 
         gw = []
         gw_tags = ("chain0", "chain2", "chain3", "chain1")
@@ -92,12 +86,12 @@ def tile_picked_ydcons_gelu_p_kernel(tc, x_words, x_scales, w1, w2, meas, offs, 
         w1_codes = [keep.tile([P, P], U32, name="w1_codes%d" % t, align_bytes=64) for t in range(PACK)]
         w1_scales = [keep.tile([P, P], U8, name="w1_scales%d" % t, align_bytes=64) for t in range(PACK)]
         w1_bf = [keep.tile([P, P, PACK], BF16, name="w1_bf%d" % t, tag="chain%d" % t, align_bytes=64) for t in range(PACK)]
-        w1_src = w1_raw[:].rearrange("p (j b g q r e) -> p g e b q j r", j=PACK, g=2, q=4, r=2, e=2)
+        w1_src = [raw[:].rearrange("p (j b g q r e) -> p g e b q j r", j=2, g=2, q=4, r=2, e=2) for raw in w1_raw]
 
         def round_w1(t, rows, copy, blocks=slice(0, H // BLOCK)):
             copy(
-                out=w1_bf[t][:].rearrange("p (b q r) j -> p b q j r", q=4, r=2)[:, blocks, :, rows, :],
-                in_=w1_src[:, t // 2, t % 2, blocks, :, rows, :],
+                out=w1_bf[t][:].rearrange("p (b q r) j -> p b q j r", q=4, r=2)[:, blocks, :, 2 * rows : 2 * rows + 2, :],
+                in_=w1_src[rows][:, t // 2, t % 2, blocks],
             )
 
         def quantize_w1(t):
@@ -107,7 +101,7 @@ def tile_picked_ydcons_gelu_p_kernel(tc, x_words, x_scales, w1, w2, meas, offs, 
                 in_=w1_bf[t][:].rearrange("p m j -> p (m j)"),
             )
 
-        first_rows, last_rows = slice(0, 2), slice(2, 4)
+        first_rows, last_rows = 0, 1
         round_w1(2, first_rows, nc.scalar.copy)
         round_w1(3, first_rows, nc.scalar.copy)
         round_w1(1, first_rows, nc.vector.tensor_copy)
@@ -122,6 +116,12 @@ def tile_picked_ydcons_gelu_p_kernel(tc, x_words, x_scales, w1, w2, meas, offs, 
         for c in range(CHUNKS):
             gather_words(c)
 
+        late = keep.tile([P, PACK * N + V], F32, name="late", tag="w1_raw0", align_bytes=64)
+        w2_rows = w2.rearrange("(b g r e) n -> g b r (e n)", g=2, r=RUN, e=2)
+        for g in range(2):
+            nc.sync.dma_start(out=late[:, 2 * g * N : 2 * (g + 1) * N], in_=w2_rows[g])
+        nc.sync.dma_start(out=late[:, PACK * N :], in_=meas)
+        nc.sync.dma_start(out=line_t[:], in_=line)
         w2_bf = keep.tile([P, N, PACK], BF16, name="w2_bf", align_bytes=64)
         w2_codes = keep.tile([P, N], U32, name="w2_codes", align_bytes=64)
         w2_scales = keep.tile([P, N], U8, name="w2_scales", align_bytes=64)

@@ -30,7 +30,7 @@ CHUNKS = S // CHUNK
 HALF = CHUNK // 2
 GROUPS = ((0, 2 * CHUNK), (2 * CHUNK, CHUNK), (3 * CHUNK, HALF), (3 * CHUNK + HALF, HALF))
 PAIRED = 2
-WARM_ROWS, WARM_PASSES = 32, 5
+WARM_ROWS, WARM_PASSES = 32, 6
 VECTOR_PICKS = 96
 
 
@@ -65,7 +65,9 @@ def tile_picked_ydcons_gelu_p_kernel(tc, x_words, x_scales, w1, w2, meas, offs, 
         nc.scalar.dma_start(out=w1_raw[0][:, :H], in_=w1_rows[:, :H])
         nc.sync.dma_start(out=xs[rows_at:, :].bitcast(I32), in_=x_scales[0].bitcast(I32))
         nc.sync.dma_start(out=w1_raw[0][:, H:], in_=w1_rows[:, H : 2 * H])
-        nc.sync.dma_start(out=w1_raw[1][:], in_=w1_rows[:, 2 * H :])
+        cut = H + H // 2
+        nc.sync.dma_start(out=w1_raw[1][:, :cut], in_=w1_rows[:, 2 * H : 2 * H + cut])
+        nc.sync.dma_start(out=w1_raw[1][:, cut:], in_=w1_rows[:, 2 * H + cut :])
         nc.sync.dma_start(out=xw[:].bitcast(I32), in_=x_words[0].rearrange("p n t -> p (n t)").bitcast(I32))
 
         nc.vector.tensor_copy(out=gs[:], in_=xs[:].indirect(offs_t[:]))
@@ -77,7 +79,7 @@ def tile_picked_ydcons_gelu_p_kernel(tc, x_words, x_scales, w1, w2, meas, offs, 
 
 
         gw = []
-        gw_tags = ("chain0", "chain2", "chain3", "chain1")
+        gw_tags = ("chain0", "chain1", "chain2", "chain3")
 
         def gather_words(c):
             gw.append(keep.tile([P, CHUNK], U32, name="gw%d" % c, tag=gw_tags[c], align_bytes=64))
@@ -94,11 +96,11 @@ def tile_picked_ydcons_gelu_p_kernel(tc, x_words, x_scales, w1, w2, meas, offs, 
                 in_=w1_src[rows][:, t // 2, t % 2, blocks],
             )
 
-        def quantize_w1(t):
+        def quantize_w1(t, columns):
             nc.vector.quantize_mx(
-                out=w1_codes[t][:].bitcast(FP8X4),
-                scales=w1_scales[t][:],
-                in_=w1_bf[t][:].rearrange("p m j -> p (m j)"),
+                out=w1_codes[t][:, columns].bitcast(FP8X4),
+                scales=w1_scales[t][:, columns],
+                in_=w1_bf[t][:, columns, :].rearrange("p m j -> p (m j)"),
             )
 
         first_rows, last_rows = 0, 1
@@ -106,13 +108,16 @@ def tile_picked_ydcons_gelu_p_kernel(tc, x_words, x_scales, w1, w2, meas, offs, 
         round_w1(3, first_rows, nc.scalar.copy)
         round_w1(1, first_rows, nc.vector.tensor_copy)
         round_w1(0, first_rows, nc.vector.tensor_copy)
-        round_w1(0, last_rows, nc.vector.tensor_copy)
-        round_w1(2, last_rows, nc.scalar.copy)
-        round_w1(1, last_rows, nc.vector.tensor_copy)
-        round_w1(3, last_rows, nc.scalar.copy, slice(0, 8))
-        round_w1(3, last_rows, nc.vector.tensor_copy, slice(8, 16))
-        for t in (0, 2, 1, 3):
-            quantize_w1(t)
+        for half in range(2):
+            blocks = slice(half * 8, (half + 1) * 8)
+            for t in range(2):
+                round_w1(t, last_rows, nc.vector.tensor_copy, blocks)
+                round_w1(2 + t, last_rows, nc.scalar.copy, blocks)
+        for half in range(2):
+            for t in range(2):
+                quantize_w1(t, slice(half * P // 2, (half + 1) * P // 2))
+        for t in range(2, PACK):
+            quantize_w1(t, slice(0, P))
         for c in range(CHUNKS):
             gather_words(c)
 

@@ -30,7 +30,7 @@ CHUNKS = S // CHUNK
 HALF = CHUNK // 2
 GROUPS = ((0, 2 * CHUNK), (2 * CHUNK, CHUNK), (3 * CHUNK, HALF), (3 * CHUNK + HALF, HALF))
 PAIRED = 2
-WARM_ROWS, WARM_PASSES = 32, 6
+WARM_ROWS, WARM_PASSES = 32, 7
 VECTOR_PICKS = 96
 
 
@@ -96,11 +96,11 @@ def tile_picked_ydcons_gelu_p_kernel(tc, x_words, x_scales, w1, w2, meas, offs, 
                 in_=w1_src[rows][:, t // 2, t % 2, blocks],
             )
 
-        def quantize_w1(t, columns):
+        def quantize_w1(t):
             nc.vector.quantize_mx(
-                out=w1_codes[t][:, columns].bitcast(FP8X4),
-                scales=w1_scales[t][:, columns],
-                in_=w1_bf[t][:, columns, :].rearrange("p m j -> p (m j)"),
+                out=w1_codes[t][:].bitcast(FP8X4),
+                scales=w1_scales[t][:],
+                in_=w1_bf[t][:].rearrange("p m j -> p (m j)"),
             )
 
         first_rows, last_rows = 0, 1
@@ -113,11 +113,8 @@ def tile_picked_ydcons_gelu_p_kernel(tc, x_words, x_scales, w1, w2, meas, offs, 
             for t in range(2):
                 round_w1(t, last_rows, nc.vector.tensor_copy, blocks)
                 round_w1(2 + t, last_rows, nc.scalar.copy, blocks)
-        for half in range(2):
-            for t in range(2):
-                quantize_w1(t, slice(half * P // 2, (half + 1) * P // 2))
-        for t in range(2, PACK):
-            quantize_w1(t, slice(0, P))
+        for t in range(PACK):
+            quantize_w1(t)
         for c in range(CHUNKS):
             gather_words(c)
 

@@ -30,7 +30,7 @@ CHUNKS = S // CHUNK
 HALF = CHUNK // 2
 GROUPS = ((0, 2 * CHUNK), (2 * CHUNK, CHUNK), (3 * CHUNK, HALF), (3 * CHUNK + HALF, HALF))
 PAIRED = 2
-WARM_ROWS, WARM_PASSES = 32, 7
+WARM_ROWS, WARM_PASSES = 32, 5
 VECTOR_PICKS = 96
 
 

@@ -30,7 +30,7 @@ CHUNKS = S // CHUNK
 HALF = CHUNK // 2
 GROUPS = ((0, 2 * CHUNK), (2 * CHUNK, CHUNK), (3 * CHUNK, HALF), (3 * CHUNK + HALF, HALF))
 PAIRED = 2
-WARM_ROWS, WARM_PASSES = 32, 5
+WARM_ROWS, WARM_PASSES = 32, 8
 VECTOR_PICKS = 96
 
 
@@ -103,6 +103,12 @@ def tile_picked_ydcons_gelu_p_kernel(tc, x_words, x_scales, w1, w2, meas, offs, 
                 in_=w1_bf[t][:].rearrange("p m j -> p (m j)"),
             )
 
+        warm_bf = keep.tile([P, PACK * CHUNK], BF16, name="warm_bf", align_bytes=64)
+        warm_codes = keep.tile([P, CHUNK], U32, name="warm_codes", align_bytes=64)
+        warm_scales = keep.tile([P, CHUNK], U8, name="warm_scales", align_bytes=64)
+        nc.scalar.copy(out=warm_bf[:], in_=w1_raw[0][:, :H])
+        nc.vector.quantize_mx(out=warm_codes[:].bitcast(FP8X4), scales=warm_scales[:], in_=warm_bf[:])
+
         first_rows, last_rows = 0, 1
         round_w1(2, first_rows, nc.scalar.copy)
         round_w1(3, first_rows, nc.scalar.copy)
@@ -137,10 +143,10 @@ def tile_picked_ydcons_gelu_p_kernel(tc, x_words, x_scales, w1, w2, meas, offs, 
         for i in range(WARM_PASSES):
             nc.tensor.matmul_mx(
                 out=idle[:],
-                lhsT=w1_codes[0][:, :WARM_ROWS].bitcast(FP8X4),
-                lhsT_scale=w1_scales[0][:, :WARM_ROWS],
-                rhs=w1_codes[0][:].bitcast(FP8X4),
-                rhs_scale=w1_scales[0][:],
+                lhsT=warm_codes[:, :WARM_ROWS].bitcast(FP8X4),
+                lhsT_scale=warm_scales[:, :WARM_ROWS],
+                rhs=warm_codes[:].bitcast(FP8X4),
+                rhs_scale=warm_scales[:],
                 start=True,
                 stop=True,
             )

@@ -65,10 +65,10 @@ def tile_picked_ydcons_gelu_p_kernel(tc, x_words, x_scales, w1, w2, meas, offs, 
         nc.scalar.dma_start(out=w1_raw[0][:, :H], in_=w1_rows[:, :H])
         nc.sync.dma_start(out=xs[rows_at:, :].bitcast(I32), in_=x_scales[0].bitcast(I32))
         nc.sync.dma_start(out=w1_raw[0][:, H:], in_=w1_rows[:, H : 2 * H])
-        cut = H + H // 2
+        cut = 2 * H - BLOCK // 2
         nc.sync.dma_start(out=w1_raw[1][:, :cut], in_=w1_rows[:, 2 * H : 2 * H + cut])
-        nc.sync.dma_start(out=w1_raw[1][:, cut:], in_=w1_rows[:, 2 * H + cut :])
         nc.sync.dma_start(out=xw[:].bitcast(I32), in_=x_words[0].rearrange("p n t -> p (n t)").bitcast(I32))
+        nc.sync.dma_start(out=w1_raw[1][:, cut:], in_=w1_rows[:, 2 * H + cut :])
 
         nc.vector.tensor_copy(out=gs[:], in_=xs[:].indirect(offs_t[:]))
         for q in range(P // QUADRANT):
@@ -114,15 +114,17 @@ def tile_picked_ydcons_gelu_p_kernel(tc, x_words, x_scales, w1, w2, meas, offs, 
         round_w1(3, first_rows, nc.scalar.copy)
         round_w1(1, first_rows, nc.vector.tensor_copy)
         round_w1(0, first_rows, nc.vector.tensor_copy)
-        for half in range(2):
-            blocks = slice(half * 8, (half + 1) * 8)
+        last_block = H // BLOCK - 1
+        for t in range(2):
+            round_w1(t, last_rows, nc.vector.tensor_copy)
+        for blocks in (slice(0, last_block), slice(last_block, last_block + 1)):
+            for t in range(2, PACK):
+                round_w1(t, last_rows, nc.scalar.copy, blocks)
+        for pair in range(2):
             for t in range(2):
-                round_w1(t, last_rows, nc.vector.tensor_copy, blocks)
-                round_w1(2 + t, last_rows, nc.scalar.copy, blocks)
-        for t in range(PACK):
-            quantize_w1(t)
-        for c in range(CHUNKS):
-            gather_words(c)
+                quantize_w1(2 * pair + t)
+            for c in range(2):
+                gather_words(2 * pair + c)
 
         late = keep.tile([P, PACK * N + V], F32, name="late", tag="w1_raw0", align_bytes=64)
         w2_rows = w2.rearrange("(b g r e) n -> g b r (e n)", g=2, r=RUN, e=2)
@@ -156,16 +158,22 @@ def tile_picked_ydcons_gelu_p_kernel(tc, x_words, x_scales, w1, w2, meas, offs, 
                 pre.append([psum.tile([P, 2, CHUNK], F32, name="pre%d_%d" % (c, g), tag="pre%d_%d" % (c, g)) for g in range(2)])
             else:
                 pre.append(psum.tile([P, PACK, CHUNK], F32, name="pre%d" % c))
-            for t in range(PACK):
-                nc.tensor.matmul_mx(
-                    out=pre[c][t // 2][:, t % 2, :] if c < PAIRED else pre[c][:, t, :],
-                    lhsT=w1_codes[t][:].bitcast(FP8X4),
-                    lhsT_scale=w1_scales[t][:],
-                    rhs=gw[c][:].bitcast(FP8X4),
-                    rhs_scale=x_plane[:, c * CHUNK : (c + 1) * CHUNK],
-                    start=True,
-                    stop=True,
-                )
+        passes = [(c, 2 * g + e) for g in range(2) for c in range(PAIRED) for e in range(2)]
+        passes = passes + [(c, t) for c in range(PAIRED, CHUNKS) for t in range(PACK)]
+        for c, t in passes:
+            nc.tensor.matmul_mx(
+                out=pre[c][t // 2][:, t % 2, :] if c < PAIRED else pre[c][:, t, :],
+                lhsT=w1_codes[t][:].bitcast(FP8X4),
+                lhsT_scale=w1_scales[t][:],
+                rhs=gw[c][:].bitcast(FP8X4),
+                rhs_scale=x_plane[:, c * CHUNK : (c + 1) * CHUNK],
+                start=True,
+                stop=True,
+            )
+        pairs = [keep.tile([P, 2, CHUNK, 2], BF16, name="pairs%d" % c, align_bytes=64) for c in range(PAIRED)]
+        for g in range(2):
+            for c in range(PAIRED):
+                nc.scalar.activation(out=pairs[c][:, g], in_=pre[c][g][:].rearrange("p e n -> p n e"), func=GELU)
 
         y_acc = [psum.tile([P, width], F32, name="y_acc%d" % g, tag="pre%d_%d" % divmod(g, 2)) for g, (first, width) in enumerate(GROUPS)]
         h_all = keep.tile([P, S], U32, name="h_all", align_bytes=64)
@@ -175,12 +183,9 @@ def tile_picked_ydcons_gelu_p_kernel(tc, x_words, x_scales, w1, w2, meas, offs, 
             c, inside = divmod(first, CHUNK)
             h_bf = keep.tile([P, width, PACK], BF16, name="h_bf%d" % first, tag="h_bf%d" % first, align_bytes=64)
             if c < PAIRED:
-                pairs = keep.tile([P, 2, width, 2], BF16, name="pairs%d" % c, align_bytes=64)
-                for g in range(2):
-                    nc.scalar.activation(out=pairs[:, g], in_=pre[c][g][:].rearrange("p e n -> p n e"), func=GELU)
                 nc.vector.tensor_copy(
                     out=h_bf[:].rearrange("p n t -> p (n t)").bitcast(F32).rearrange("p (m u g) -> p m g u", g=2, u=2),
-                    in_=pairs[:].rearrange("p g n e -> p (g n e)").bitcast(F32).rearrange("p (g m u) -> p m g u", g=2, u=2),
+                    in_=pairs[c][:].rearrange("p g n e -> p (g n e)").bitcast(F32).rearrange("p (g m u) -> p m g u", g=2, u=2),
                 )
             else:
                 nc.scalar.activation(out=h_bf[:], in_=pre[c][:, :, inside : inside + width].rearrange("p t n -> p n t"), func=GELU)

from contextlib import ExitStack

import concourse.mybir as mybir

K, T, S, H, N, V = 512, 1024, 512, 512, 128, 256
FLOPS = 2 * K * H * S + 2 * H * N * S

F32 = mybir.dt.float32
BF16 = mybir.dt.bfloat16
I32 = mybir.dt.int32
U32 = mybir.dt.uint32
U16 = mybir.dt.uint16
U8 = mybir.dt.uint8
FP8X4 = mybir.dt.float8_e4m3fn_x4
GELU = mybir.ActivationFunctionType.Gelu_apprx_tanh
COPY = mybir.ActivationFunctionType.Copy
ADD = mybir.AluOpType.add
MULT = mybir.AluOpType.mult

P = 128
QUADRANT = 32
PACK = 4
BLOCK = 32
RUN = BLOCK // PACK
SCALE_ROWS = K // BLOCK
LINE_WORDS = 4
PER_COLUMN = 16
CHUNK = 128
CHUNKS = S // CHUNK
HALF = CHUNK // 2
GROUPS = ((0, 2 * CHUNK), (2 * CHUNK, CHUNK), (3 * CHUNK, HALF), (3 * CHUNK + HALF, HALF))
PAIRED = 2
WARM_ROWS, WARM_PASSES = 32, 8
VECTOR_PICKS = 96


def tile_picked_ydcons_gelu_p_kernel(tc, x_words, x_scales, w1, w2, meas, offs, line, out):
    nc = tc.nc
    with ExitStack() as ctx:
        keep = ctx.enter_context(tc.tile_pool(name="keep", bufs=1))
        psum = ctx.enter_context(tc.psum_pool(name="psum", bufs=1))

        offs_t = keep.tile([P, S // PER_COLUMN], U16, name="offs_t")
        line_t = keep.tile([P, V // PER_COLUMN], U16, name="line_t")
        xw = keep.tile([P, T], U32, name="xw", align_bytes=64)
        xs = keep.tile([P, T], U8, name="xs", align_bytes=64)
        gs = keep.tile([P, S], U8, name="gs", align_bytes=64)
        x_plane = keep.tile([P, S], U8, name="x_plane", align_bytes=64)
        w1_raw = [keep.tile([P, 2 * H], F32, name="w1_raw%d" % i, tag="w1_raw%d" % i, align_bytes=64) for i in range(2)]

        def offs_slice(first, count):
            return offs_t[:, first // PER_COLUMN : (first + count) // PER_COLUMN]

        rows_at = P - SCALE_ROWS
        nc.vector.memset(xs[:rows_at, :].bitcast(I32), 0)
        nc.vector.memset(x_plane[:].bitcast(I32), 0)
        quarter = keep.tile([P, VECTOR_PICKS], F32, name="quarter", align_bytes=64)
        nc.vector.memset(quarter[:], 0.25)

        warm = keep.tile([P, 1], F32, name="warm")
        nc.scalar.activation(out=warm[:], in_=quarter[:, :1], func=GELU)

        w1_rows = w1.rearrange("(p j) c -> p (j c)", j=PACK)
        nc.sync.dma_start(out=offs_t[:], in_=offs)
        nc.scalar.dma_start(out=w1_raw[0][:, :H], in_=w1_rows[:, :H])
        nc.sync.dma_start(out=xs[rows_at:, :].bitcast(I32), in_=x_scales[0].bitcast(I32))
        nc.sync.dma_start(out=w1_raw[0][:, H:], in_=w1_rows[:, H : 2 * H])
        cut = 2 * H - BLOCK // 2
        nc.sync.dma_start(out=w1_raw[1][:, :cut], in_=w1_rows[:, 2 * H : 2 * H + cut])
        nc.sync.dma_start(out=xw[:].bitcast(I32), in_=x_words[0].rearrange("p n t -> p (n t)").bitcast(I32))
        nc.sync.dma_start(out=w1_raw[1][:, cut:], in_=w1_rows[:, 2 * H + cut :])

        nc.vector.tensor_copy(out=gs[:], in_=xs[:].indirect(offs_t[:]))
        for q in range(P // QUADRANT):
            nc.sync.dma_start(
                out=x_plane[q * QUADRANT : q * QUADRANT + PACK, :].bitcast(I32),
                in_=gs[rows_at + q * PACK : rows_at + (q + 1) * PACK, :].bitcast(I32),
            )


        gw = []
        gw_tags = ("chain0", "chain1", "chain2", "chain3")

        def gather_words(c):
            gw.append(keep.tile([P, CHUNK], U32, name="gw%d" % c, tag=gw_tags[c], align_bytes=64))
            nc.vector.tensor_copy(out=gw[c][:], in_=xw[:].indirect(offs_slice(c * CHUNK, CHUNK)))

        w1_codes = [keep.tile([P, P], U32, name="w1_codes%d" % t, align_bytes=64) for t in range(PACK)]
        w1_scales = [keep.tile([P, P], U8, name="w1_scales%d" % t, align_bytes=64) for t in range(PACK)]
        w1_bf = [keep.tile([P, P, PACK], BF16, name="w1_bf%d" % t, tag="chain%d" % t, align_bytes=64) for t in range(PACK)]
        w1_src = [raw[:].rearrange("p (j b g q r e) -> p g e b q j r", j=2, g=2, q=4, r=2, e=2) for raw in w1_raw]

        def round_w1(t, rows, copy, blocks=slice(0, H // BLOCK)):
            copy(
                out=w1_bf[t][:].rearrange("p (b q r) j -> p b q j r", q=4, r=2)[:, blocks, :, 2 * rows : 2 * rows + 2, :],
                in_=w1_src[rows][:, t // 2, t % 2, blocks],
            )

        def quantize_w1(t):
            nc.vector.quantize_mx(
                out=w1_codes[t][:].bitcast(FP8X4),
                scales=w1_scales[t][:],
                in_=w1_bf[t][:].rearrange("p m j -> p (m j)"),
            )

        warm_bf = keep.tile([P, PACK * CHUNK], BF16, name="warm_bf", align_bytes=64)
        warm_codes = keep.tile([P, CHUNK], U32, name="warm_codes", align_bytes=64)
        warm_scales = keep.tile([P, CHUNK], U8, name="warm_scales", align_bytes=64)
        nc.scalar.copy(out=warm_bf[:], in_=w1_raw[0][:, :H])
        nc.vector.quantize_mx(out=warm_codes[:].bitcast(FP8X4), scales=warm_scales[:], in_=warm_bf[:])

        first_rows, last_rows = 0, 1
        round_w1(2, first_rows, nc.scalar.copy)
        round_w1(3, first_rows, nc.scalar.copy)
        round_w1(1, first_rows, nc.vector.tensor_copy)
        round_w1(0, first_rows, nc.vector.tensor_copy)
        last_block = H // BLOCK - 1
        for t in range(2):
            round_w1(t, last_rows, nc.vector.tensor_copy)
        for blocks in (slice(0, last_block), slice(last_block, last_block + 1)):
            for t in range(2, PACK):
                round_w1(t, last_rows, nc.scalar.copy, blocks)
        for pair in range(2):
            for t in range(2):
                quantize_w1(2 * pair + t)
            for c in range(2):
                gather_words(2 * pair + c)

        late = keep.tile([P, PACK * N + V], F32, name="late", tag="w1_raw0", align_bytes=64)
        w2_rows = w2.rearrange("(b g r e) n -> g b r (e n)", g=2, r=RUN, e=2)
        for g in range(2):
            nc.sync.dma_start(out=late[:, 2 * g * N : 2 * (g + 1) * N], in_=w2_rows[g])
        nc.sync.dma_start(out=late[:, PACK * N :], in_=meas)
        nc.sync.dma_start(out=line_t[:], in_=line)
        w2_bf = keep.tile([P, N, PACK], BF16, name="w2_bf", align_bytes=64)
        w2_codes = keep.tile([P, N], U32, name="w2_codes", align_bytes=64)
        w2_scales = keep.tile([P, N], U8, name="w2_scales", align_bytes=64)
        nc.vector.tensor_copy(
            out=w2_bf[:].rearrange("p (m u) t -> p m t u", u=LINE_WORDS),
            in_=late[:, : PACK * N].rearrange("p (t m u) -> p m t u", t=PACK, u=LINE_WORDS),
        )
        nc.vector.quantize_mx(out=w2_codes[:].bitcast(FP8X4), scales=w2_scales[:], in_=w2_bf[:].rearrange("p n t -> p (n t)"))

        idle = psum.tile([WARM_ROWS, CHUNK], F32, name="idle")
        for i in range(WARM_PASSES):
            nc.tensor.matmul_mx(
                out=idle[:],
                lhsT=warm_codes[:, :WARM_ROWS].bitcast(FP8X4),
                lhsT_scale=warm_scales[:, :WARM_ROWS],
                rhs=warm_codes[:].bitcast(FP8X4),
                rhs_scale=warm_scales[:],
                start=True,
                stop=True,
            )
        pre = []
        for c in range(CHUNKS):
            if c < PAIRED:
                pre.append([psum.tile([P, 2, CHUNK], F32, name="pre%d_%d" % (c, g), tag="pre%d_%d" % (c, g)) for g in range(2)])
            else:
                pre.append(psum.tile([P, PACK, CHUNK], F32, name="pre%d" % c))
        passes = [(c, 2 * g + e) for g in range(2) for c in range(PAIRED) for e in range(2)]
        passes = passes + [(c, t) for c in range(PAIRED, CHUNKS) for t in range(PACK)]
        for c, t in passes:
            nc.tensor.matmul_mx(
                out=pre[c][t // 2][:, t % 2, :] if c < PAIRED else pre[c][:, t, :],
                lhsT=w1_codes[t][:].bitcast(FP8X4),
                lhsT_scale=w1_scales[t][:],
                rhs=gw[c][:].bitcast(FP8X4),
                rhs_scale=x_plane[:, c * CHUNK : (c + 1) * CHUNK],
                start=True,
                stop=True,
            )
        pairs = [keep.tile([P, 2, CHUNK, 2], BF16, name="pairs%d" % c, align_bytes=64) for c in range(PAIRED)]
        for g in range(2):
            for c in range(PAIRED):
                nc.scalar.activation(out=pairs[c][:, g], in_=pre[c][g][:].rearrange("p e n -> p n e"), func=GELU)

        y_acc = [psum.tile([P, width], F32, name="y_acc%d" % g, tag="pre%d_%d" % divmod(g, 2)) for g, (first, width) in enumerate(GROUPS)]
        h_all = keep.tile([P, S], U32, name="h_all", align_bytes=64)
        h_scales_all = keep.tile([P, S], U8, name="h_scales_all", align_bytes=64)

        def hidden(first, width):
            c, inside = divmod(first, CHUNK)
            h_bf = keep.tile([P, width, PACK], BF16, name="h_bf%d" % first, tag="h_bf%d" % first, align_bytes=64)
            if c < PAIRED:
                nc.vector.tensor_copy(
                    out=h_bf[:].rearrange("p n t -> p (n t)").bitcast(F32).rearrange("p (m u g) -> p m g u", g=2, u=2),
                    in_=pairs[c][:].rearrange("p g n e -> p (g n e)").bitcast(F32).rearrange("p (g m u) -> p m g u", g=2, u=2),
                )
            else:
                nc.scalar.activation(out=h_bf[:], in_=pre[c][:, :, inside : inside + width].rearrange("p t n -> p n t"), func=GELU)
            nc.vector.quantize_mx(
                out=h_all[:, first : first + width].bitcast(FP8X4),
                scales=h_scales_all[:, first : first + width],
                in_=h_bf[:].rearrange("p n t -> p (n t)"),
            )

        for g, (first, width) in enumerate(GROUPS):
            for piece in range(first, first + width, CHUNK):
                hidden(piece, min(width, CHUNK))
            nc.tensor.matmul_mx(
                out=y_acc[g][:],
                lhsT=w2_codes[:].bitcast(FP8X4),
                lhsT_scale=w2_scales[:],
                rhs=h_all[:, first : first + width].bitcast(FP8X4),
                rhs_scale=h_scales_all[:, first : first + width],
                start=True,
                stop=True,
            )

        meas75 = keep.tile([P, V], F32, name="meas75", tag="h_bf%d" % (S - HALF), align_bytes=64)
        nc.vector.tensor_scalar_mul(out=meas75[:], in0=late[:, PACK * N :], scalar1=0.75)

        y = keep.tile([P, S], F32, name="y", align_bytes=64)
        for g, (first, width) in enumerate(GROUPS):
            copy = nc.vector.tensor_copy if g == 2 else nc.scalar.copy
            copy(out=y[:, first : first + width], in_=y_acc[g][:])

        picked = keep.tile([P, V], F32, name="picked", align_bytes=64)
        split = VECTOR_PICKS // PER_COLUMN
        nc.vector.tensor_tensor(out=picked[:, :VECTOR_PICKS], in0=y[:].indirect(line_t[:, :split]), in1=quarter[:], op=MULT)
        nc.scalar.activation(out=picked[:, VECTOR_PICKS:], in_=y[:].indirect(line_t[:, split:]), func=COPY, scale=0.25)
        nc.vector.tensor_tensor(out=y[:].indirect(line_t[:]), in0=picked[:], in1=meas75[:], op=ADD)
        nc.sync.dma_start(out=out, in_=y[:])
